import numpy as np, ml_dtypes
CORES = [5,21,45,77,85,101,109,125,133,141,189,213]
N = 12
S, T = 4096, 256
def entries(a): return a.T.reshape(-1)
def pack(v, P): return np.ascontiguousarray(np.asarray(v, np.int32).reshape(-1, P).T)
def lists(rng, how):
    M = rng.integers(0, S, (N, S)); b = rng.integers(0, S, T)
    if how == "alike": M = np.stack([rng.permutation(S) for f in range(N)]); b[:] = rng.integers(S)
    if how == "edge":
        M = np.where(rng.random((N, S)) < 0.5, 0, S - 1); w = rng.permutation(N) % 2 * (S - 1); M[:, 0] = w; M[:, S - 1] = S - 1 - w
        b = np.where(rng.random(T) < 0.5, 0, S - 1); b[rng.permutation(T)[:2]] = [0, S - 1]
    if how == "fold":
        V = np.stack([rng.permutation(S)[:4] for f in range(N + 1)]); M = V[np.arange(N)[:, None], rng.integers(0, 4, (N, S))]
        M[np.arange(N)[:, None], V[1:]] = V[:N]; b[rng.permutation(T)[:4]] = V[N]
    if how == "mixed":
        k = np.concatenate([[3, 3], rng.permutation(np.arange(N - 2) % 3)])
        for f in range(N): M[f] = [np.arange(S), rng.permutation(S), M[f], rng.integers(0, S, 4)[rng.integers(0, 4, S)]][k[f]]
    if how == "turn": M = np.stack([rng.permutation(S) for f in range(N)]); b = rng.permutation(S)[:T]
    return {"bp": np.stack([pack(m, 16) for m in M]), "st": np.broadcast_to(pack(b, 16), (N, 16, T // 16)).copy()}
def setup_inputs(rng):
    return dict({"tab": rng.standard_normal((N, 128, S), dtype=np.float32).astype(ml_dtypes.bfloat16)}, **lists(rng, "uniform"))
def setup_inputs_alike(rng):
    d = setup_inputs(rng); d.update(lists(rng, "alike"))
    for k in ("tab",): d[k] = (d[k].astype(np.float32) * 1048576.0).astype(d[k].dtype)
    return d
def setup_inputs_edge(rng):
    d = setup_inputs(rng); d.update(lists(rng, "edge"))
    for k in ("tab",): d[k] = (d[k].astype(np.float32) * (1 / 1024.0)).astype(d[k].dtype)
    return d
def setup_inputs_fold(rng):
    d = setup_inputs(rng); d.update(lists(rng, "fold"))
    return d
def setup_inputs_mixed(rng):
    d = setup_inputs(rng); d.update(lists(rng, "mixed"))
    return d
def setup_inputs_turn(rng):
    d = setup_inputs(rng); d.update(lists(rng, "turn"))
    return d
def check_inputs(x):
    bad = []
    if x["bp"].min() < 0 or x["bp"].max() >= S: bad.append("bp out of range")
    if x["st"].min() < 0 or x["st"].max() >= S: bad.append("st out of range")
    if not all(np.array_equal(a, x["st"][0]) for a in x["st"]): bad.append("st isn't alike on all ranks")
    return bad
def reference(tab, bp, st):
    b = entries(st[0]); y = np.zeros((N, 128, T), tab.dtype)
    for f in range(N - 1, -1, -1):
        y[f] = tab[f][:, b]
        b = entries(bp[f])[b]
    return {"y": y}

@@ -1,0 +1,326 @@
+from concourse.bass import DstId, RemoteDMATransfer
+from concourse.mybir import AluOpType as Op, ActivationFunctionType as Act
+
+N = 12
+TOP = N - 1
+SCRATCH = {
+    "land": ("sbuf", [128, 64 * N], "bfloat16"),
+    "win": ("sbuf", [128, 512 * N], "bfloat16"),
+    "tb": ("sbuf", [128, 4096], "bfloat16"),
+}
+for _name, _w, _t in (
+        ("raw", 32, "int32"), ("sp", 64, "int32"), ("mp", 64, "bfloat16"), ("pidx", 1, "int32"),
+        ("pgr", 2, "int32"), ("col", 2, "float32"), ("pk", 8, "float32"), ("i_r", 128, "bfloat16"),
+        ("i_g", 128, "bfloat16"), ("rp", 1024, "bfloat16"), ("bd", 128, "bfloat16"), ("bd8", 128, "bfloat16"),
+        ("ex", 128, "float32"), ("dg", 32, "bfloat16"), ("ct1", 32, "float32"), ("ct2", 32, "float32"),
+        ("ct", 32, "float32"), ("r1", 1, "float32"), ("sd", 32, "float32"), ("sc1", 1, "float32"),
+        ("scl", 1, "float32"), ("gm", 8, "float32"), ("wr", 2, "int32"), ("wsp", 4, "int32"),
+        ("lof", 2, "float32"), ("rl", 32, "bfloat16"), ("offs", 2, "uint16"), ("mk", 64, "bfloat16"),
+        ("xl", 32, "bfloat16"), ("xh", 32, "bfloat16"), ("scn", 32, "float32"), ("ys", 32, "float32"),
+        ("z", 32, "float32"), ("s2", 32, "float32"), ("rr", 16, "float32"), ("fo", 16, "uint16"),
+        ("ya", 128, "bfloat16"), ("yb", 128, "bfloat16")):
+    SCRATCH[_name] = ("sbuf", [128, _w], _t)
+for _name in ("p_l", "p_h", "p_f", "p_r0", "p_r1", "p_r2", "p_r3"):
+    SCRATCH[_name] = ("psum", [128, 512], "float32")
+SEMAPHORES = ["v", "pe", "a", "gi", "dbp", "dst", "dtab", "dya", "dyb", "sa", "sb"] + ["m%d" % _m for _m in range(1, N)]
+
+
+def land(T, m):
+    return T.land[:, 64 * m:64 * m + 64]
+
+
+def win(T, m, a, b):
+    return T.win[:, 512 * m + a:512 * m + b]
+
+
+def bits(mask):
+    return bin(mask).count("1")
+
+
+def relay_of(src, dsts, topo, ncores):
+    for c in range(ncores):
+        if c != src and topo.host(c) == topo.host(src) and topo.chip(c) == topo.chip(src) \
+                and topo.die(c) == topo.die(src) and all(topo.may_write(c, d) for d in dsts):
+            return c
+    raise ValueError("no relay")
+
+
+def plan(f, cores, topo):
+    src = cores[f]
+    straight = [d for d in range(f) if topo.may_write(src, cores[d])]
+    other = [d for d in range(f) if not topo.may_write(src, cores[d])]
+    relay = relay_of(src, [cores[d] for d in other], topo, 256) if other else None
+    return straight, other, relay
+
+
+def send(g, src, dsts, f, T, topo, mask, local_sem):
+    ids = []
+    for d in dsts:
+        rid, pid = topo.addr(d, src)
+        ids.append(DstId(rid=rid, pnc=pid))
+    g.remote_dma_fused([RemoteDMATransfer(dst_ids=ids, dma_engine_mask=mask, remote_sem=T.sem["m%d" % f],
+                                          srcs=[land(T, f)], dsts=[land(T, f) for d in dsts])],
+                       local_sem=local_sem)
+    return bits(mask)
+
+
+def pairs(lst):
+    return [lst[i:i + 2] for i in range(0, len(lst), 2)]
+
+
+def run_relay(g, core, f, other, T, topo):
+    cores = list(T.cores)
+    off = topo.mask(core, cores[other[0]])
+    g.wait_ge(T.sem["m%d" % f], bits(off))
+    if 0 in other:
+        groups = [[d] for d in other[:2]] + pairs(other[2:])
+    else:
+        groups = pairs(other)
+    n = 0
+    for grp in groups:
+        n += send(g, core, [cores[d] for d in grp], f, T, topo, off, T.sem.sa)
+    g.wait_ge(T.sem.sa, n)
+
+
+def rank_program(g, core, T, topo):
+    cores = list(T.cores)
+    f = T.rank_of(core)
+    if f is None:
+        for r in range(1, N):
+            straight, other, relay = plan(r, cores, topo)
+            if relay == core:
+                run_relay(g, core, r, other, T, topo)
+        return
+
+    sem = T.sem
+    straight, other, relay = plan(f, cores, topo)
+    cnt = {"v": 0, "pe": 0, "a": 0, "gi": 0}
+    V, PE, A = g.vector, g.tensor, g.scalar
+
+    def done(key, ins):
+        ins.then_inc(sem[key], 1)
+        cnt[key] += 1
+        return cnt[key]
+
+    def ts(out, in0, s1, s2, *ops):
+        return done("v", V.tensor_scalar(out, in0, s1, s2, *ops))
+
+    def vw(n):
+        V.wait_ge(sem.v, n)
+
+    if f > 0:
+        g.sync.dma_start(T.raw[:, :], T.bp[:, :]).then_inc(sem.dbp, 16)
+    if f == TOP:
+        for k in range(8):
+            q = A if k % 2 else g.sync
+            q.dma_start(T.wr[16 * k:16 * k + 16, :], T.st[:, 2 * k:2 * k + 2]).then_inc(sem.dst, 16)
+
+    done("gi", g.iota(T.pidx[:, :], [[0, 1]], 0, 1))
+    done("gi", g.iota(T.pk[:, :], [[-1, 8]], 0, 1, allow_small_or_imprecise_dtypes=True))
+    done("gi", g.iota(T.i_r[:, :], [[0, 8], [1, 16]], 0, 0, allow_small_or_imprecise_dtypes=True))
+    done("gi", g.iota(T.i_g[:, :], [[1, 8], [0, 16]], 0, 0, allow_small_or_imprecise_dtypes=True))
+    V.wait_ge(sem.gi, 4)
+    ts(T.pgr[:, 0:1], T.pidx[:, :], 4, None, Op.arith_shift_right)
+    ts(T.pgr[:, 1:2], T.pidx[:, :], 15, None, Op.bitwise_and)
+    for k in range(8):
+        n_rp = ts(T.rp[:, 128 * k:128 * k + 128], T.i_r[:, :], 8.0, T.pk[:, k:k + 1], Op.mult, Op.is_equal)
+    vw(n_rp)
+    n_col = done("v", V.tensor_copy(T.col[:, :], T.pgr[:, :]))
+
+    n_prep = 0
+    if f > 0:
+        V.wait_ge(sem.dbp, 16)
+        ts(T.sp[:, 0:64:2], T.raw[:, :], 3, 510, Op.arith_shift_right, Op.bitwise_and)
+        n = ts(T.sp[:, 1:64:2], T.raw[:, :], 15, None, Op.bitwise_and)
+        vw(n)
+        n_prep = done("v", V.tensor_copy(T.mp[:, :] if f == TOP else land(T, f), T.sp[:, :]))
+
+    state = {"sa": 0, "sb": 0}
+
+    def sends(ready):
+        for key, val in ready:
+            g.wait_ge(sem[key], val)
+        if relay is not None:
+            off = topo.mask(relay, cores[other[0]])
+            state["sa"] += send(g, core, [relay], f, T, topo, off, sem.sa)
+        for i, grp in enumerate(pairs(straight)):
+            key = "sa" if i == 0 else "sb"
+            state[key] += send(g, core, [cores[d] for d in grp], f, T, topo,
+                               topo.mask(core, cores[grp[0]]), sem[key])
+
+    if 0 < f < TOP:
+        sends([("v", n_prep)])
+
+    pg, pr = T.col[:, 0:1], T.col[:, 1:2]
+    i32 = T.i_r[:, 0:32]
+    vw(n_col)
+    ts(T.bd[:, :], T.i_g[:, :], pg, None, Op.is_equal)
+    ts(T.bd8[:, :], T.i_g[:, :], pg, 8.0, Op.is_equal, Op.mult)
+    ts(T.dg[:, :], i32, pr, None, Op.is_equal)
+    n = ts(T.r1[:, :], pr, 1.0, None, Op.add)
+    vw(n)
+    ts(T.ct1[:, :], T.dg[:, :], -1.0, 1.0, Op.mult, Op.add)
+    ts(T.sc1[:, :], pr, 15.0, 1.0 - 2.0 ** -14, Op.is_equal, Op.mult)
+    n = ts(T.ct2[:, :], i32, T.r1[:, :], 16383.0, Op.is_equal, Op.mult)
+    vw(n)
+    done("v", V.tensor_tensor(T.ct[:, :], T.ct1[:, :], T.ct2[:, :], Op.add))
+    ts(T.scl[:, :], T.sc1[:, :], 2.0 ** -14, None, Op.add)
+    ts(T.sd[:, :], i32, 0.0, None, Op.not_equal)
+    ts(T.gm[:, :], T.i_g[:, 0:128:16], pg, None, Op.is_equal)
+    n_const = ts(T.ex[:, :], T.i_r[:, :], pr, None, Op.is_equal)
+
+    banks = {"next": 0}
+    bank_free = [0, 0, 0, 0]
+    wready = {}
+
+    def spread(m, src, waitsem, val):
+        PE.wait_ge(sem[waitsem], val)
+        n_a = 0
+        for h in range(2):
+            b = banks["next"]
+            banks["next"] = (b + 1) % 4
+            if bank_free[b]:
+                PE.wait_ge(sem.a, bank_free[b])
+            ps = T["p_r%d" % b]
+            n_pe = 0
+            for k in range(4):
+                kk = 4 * h + k
+                n_pe = done("pe", PE.matmul(ps[:, 64 * k:64 * k + 64], T.rp[:, 128 * kk:128 * kk + 128],
+                                            src, True, True))
+            A.wait_ge(sem.pe, n_pe)
+            n_a = done("a", A.activation(win(T, m, 256 * h, 256 * h + 256), ps[:, 0:256], Act.Copy))
+            bank_free[b] = n_a
+        wready[m] = n_a
+
+    turn = {"mk": 0}
+
+    def mask_of():
+        return T.mk[:, 32 * turn["mk"]:32 * turn["mk"] + 32]
+
+    def new_mask(lo_row):
+        turn["mk"] = 1 - turn["mk"]
+        return ts(mask_of(), lo_row, pr, None, Op.is_equal)
+
+    def gathers(m, n_state):
+        V.wait_ge(sem.a, wready[m])
+        vw(n_state)
+        o = T.offs[:, 0:2]
+        nl = done("v", V.tensor_tensor(T.xl[:, :], win(T, m, 1, 512).indirect(o), mask_of(), Op.mult))
+        nh = done("v", V.tensor_tensor(T.xh[:, :], win(T, m, 0, 511).indirect(o), mask_of(), Op.mult))
+        return nl, nh
+
+    def add_up(nl, nh):
+        PE.wait_ge(sem.v, nl)
+        a = done("pe", PE.matmul(T.p_l[:, 0:32], T.bd[:, :], T.xl[:, :], True, True))
+        PE.wait_ge(sem.v, nh)
+        b = done("pe", PE.matmul(T.p_h[:, 0:32], T.bd[:, :], T.xh[:, :], True, True))
+        return a, b
+
+    def next_state(lo_row, hi_row, nl=0, nh=0):
+        if nl:
+            V.wait_ge(sem.pe, nl)
+        new_mask(lo_row)
+        if nh:
+            V.wait_ge(sem.pe, nh)
+        n1 = done("v", V.tensor_tensor_scan(T.scn[:, :], T.ct[:, :], hi_row, 0.0, Op.mult, Op.add))
+        vw(n1)
+        return ts(T.offs[:, :], T.scn[:, 15:32:16], T.scl[:, :], None, Op.mult)
+
+    hi_pay = T.land[:, 64 * TOP:64 * TOP + 32]
+    lo_pay = T.land[:, 64 * TOP + 32:64 * TOP + 64]
+    if f == TOP:
+        V.wait_ge(sem.dst, 128)
+        ts(T.wsp[:, 0:2], T.wr[:, :], 3, 510, Op.arith_shift_right, Op.bitwise_and)
+        n = ts(T.wsp[:, 2:4], T.wr[:, :], 15, None, Op.bitwise_and)
+        vw(n)
+        done("v", V.tensor_copy(T.lof[:, :], T.wsp[:, 2:4]))
+        n = done("v", V.tensor_copy(T.offs[:, :], T.wsp[:, 0:2]))
+        vw(n)
+        ts(T.rl[:, 0:16], T.dg[:, 0:16], T.lof[:, 0:1], None, Op.mult)
+        n_rl = ts(T.rl[:, 16:32], T.dg[:, 16:32], T.lof[:, 1:2], None, Op.mult)
+        spread(TOP, T.mp[:, :], "v", n_prep)
+        PE.wait_ge(sem.v, n_rl)
+        n_l = done("pe", PE.matmul(T.p_l[:, 0:32], T.bd[:, :], T.rl[:, :], True, True))
+        V.wait_ge(sem.pe, n_l)
+        n = new_mask(T.p_l[:, 0:32])
+        nl, nh = gathers(TOP, n)
+        a, b = add_up(nl, nh)
+        V.wait_ge(sem.pe, a)
+        n_v = done("v", V.tensor_copy(lo_pay, T.p_l[:, 0:32]))
+        A.wait_ge(sem.pe, b)
+        n_a = done("a", A.activation(hi_pay, T.p_h[:, 0:32], Act.Copy))
+        sends([("v", n_v), ("a", n_a)])
+        n_s2 = done("v", V.tensor_copy(T.s2[:, 15:32:16], T.wr[:, :]))
+    else:
+        arrived = bits(topo.mask(cores[TOP], cores[0]))
+        if f < TOP - 1:
+            maps = list(range(TOP - 1, f, -1))
+            late = [m for m in maps if not topo.may_write(cores[m], core)]
+            PE.wait_ge(sem.v, n_rp)
+            for m in maps:
+                if m not in late:
+                    spread(m, land(T, m), "m%d" % m, arrived)
+            V.wait_ge(sem["m%d" % TOP], arrived)
+            vw(n_const)
+            n_state = next_state(lo_pay, hi_pay)
+            nl = nh = 0
+            for m in maps:
+                while m not in wready:
+                    x = late.pop(0)
+                    spread(x, land(T, x), "m%d" % x, arrived)
+                nl, nh = gathers(m, n_state)
+                if m > f + 1:
+                    a, b = add_up(nl, nh)
+                    n_state = next_state(T.p_l[:, 0:32], T.p_h[:, 0:32], a, b)
+                    if late:
+                        x = late.pop(0)
+                        spread(x, land(T, x), "m%d" % x, arrived)
+            PE.wait_ge(sem.v, nl)
+            done("pe", PE.matmul(T.p_f[:, 0:32], T.bd[:, :], T.xl[:, :], True, False))
+            PE.wait_ge(sem.v, nh)
+            n = done("pe", PE.matmul(T.p_f[:, 0:32], T.bd8[:, :], T.xh[:, :], False, True))
+            V.wait_ge(sem.pe, n)
+            row = T.p_f[:, 0:32]
+        else:
+            V.wait_ge(sem["m%d" % TOP], arrived)
+            vw(n_const)
+            n = ts(T.ys[:, :], hi_pay, 8.0, None, Op.mult)
+            vw(n)
+            n = done("v", V.tensor_tensor(T.z[:, :], T.ys[:, :], lo_pay, Op.add))
+            vw(n)
+            row = T.z[:, :]
+        n = done("v", V.tensor_tensor(T.ys[:, :], row, T.dg[:, :], Op.mult))
+        vw(n)
+        n_s2 = done("v", V.tensor_tensor_scan(T.s2[:, :], T.sd[:, :], T.ys[:, :], 0.0, Op.mult, Op.add))
+
+    vw(n_s2)
+    ts(T.rr[:, 0:16:2], T.gm[:, :], T.s2[:, 15:16], None, Op.mult)
+    n = ts(T.rr[:, 1:16:2], T.gm[:, :], T.s2[:, 31:32], None, Op.mult)
+    PE.wait_ge(sem.v, n)
+    n = done("pe", PE.matmul(T.p_f[:, 0:16], T.ex[:, :], T.rr[:, :], True, True))
+    V.wait_ge(sem.pe, n)
+    n_fo = done("v", V.tensor_copy(T.fo[:, :], T.p_f[:, 0:16]))
+
+    if state["sa"]:
+        g.sync.wait_ge(sem.sa, state["sa"])
+    g.sync.dma_start(T.tb[:, :], T.tab[:, :]).then_inc(sem.dtab, 16)
+
+    V.wait_ge(sem.dtab, 16)
+    vw(n_fo)
+    n_ya = done("v", V.tensor_copy(T.ya[:, :], T.tb[:, :].indirect(T.fo[:, 0:8])))
+    A.wait_ge(sem.dtab, 16)
+    A.wait_ge(sem.v, n_fo)
+    n_yb = done("a", A.activation(T.yb[:, :], T.tb[:, :].indirect(T.fo[:, 8:16]), Act.Copy))
+    g.sync.wait_ge(sem.v, n_ya)
+    g.sync.dma_start(T.y[:, 0:128], T.ya[:, :]).then_inc(sem.dya, 16)
+    A.wait_ge(sem.a, n_yb)
+    A.dma_start(T.y[:, 128:256], T.yb[:, :]).then_inc(sem.dyb, 16)
+
+    for key in ("v", "pe", "a"):
+        if cnt[key]:
+            g.wait_ge(sem[key], cnt[key])
+    for key in ("sa", "sb"):
+        if state[key]:
+            g.wait_ge(sem[key], state[key])
+    g.wait_ge(sem.dya, 16)
+    g.wait_ge(sem.dyb, 16)

@@ -9,20 +9,19 @@ SCRATCH = {
     "tb": ("sbuf", [128, 4096], "bfloat16"),
 }
 for _name, _w, _t in (
-        ("raw", 32, "int32"), ("sp", 64, "int32"), ("mp", 64, "bfloat16"), ("pidx", 1, "int32"),
-        ("pgr", 2, "int32"), ("col", 2, "float32"), ("pk", 8, "float32"), ("i_r", 128, "bfloat16"),
-        ("i_g", 128, "bfloat16"), ("rp", 1024, "bfloat16"), ("bd", 128, "bfloat16"), ("bd8", 128, "bfloat16"),
-        ("ex", 128, "float32"), ("dg", 32, "bfloat16"), ("ct1", 32, "float32"), ("ct2", 32, "float32"),
-        ("ct", 32, "float32"), ("r1", 1, "float32"), ("sd", 32, "float32"), ("sc1", 1, "float32"),
-        ("scl", 1, "float32"), ("gm", 8, "float32"), ("wr", 2, "int32"), ("wsp", 4, "int32"),
-        ("lof", 2, "float32"), ("rl", 32, "bfloat16"), ("offs", 2, "uint16"), ("mk", 64, "bfloat16"),
-        ("xl", 32, "bfloat16"), ("xh", 32, "bfloat16"), ("scn", 32, "float32"), ("ys", 32, "float32"),
-        ("z", 32, "float32"), ("s2", 32, "float32"), ("rr", 16, "float32"), ("fo", 16, "uint16"),
+        ("raw", 32, "int32"), ("sp", 64, "int32"), ("pidx", 1, "int32"), ("pgr", 2, "int32"),
+        ("col", 2, "float32"), ("pk", 8, "float32"), ("i_r", 128, "bfloat16"), ("i_g", 128, "bfloat16"),
+        ("rp", 1024, "bfloat16"), ("bd", 128, "bfloat16"), ("ex", 128, "bfloat16"), ("ex8", 128, "bfloat16"),
+        ("dg", 32, "bfloat16"), ("ct1", 32, "float32"), ("ct2", 32, "float32"), ("ct", 32, "float32"),
+        ("r1", 1, "float32"), ("sc1", 1, "float32"), ("scl", 1, "float32"), ("gs", 8, "bfloat16"),
+        ("wr", 16, "int32"), ("wsp", 32, "int32"), ("lof", 2, "float32"), ("rl", 32, "bfloat16"),
+        ("offs", 2, "uint16"), ("mk", 32, "bfloat16"), ("xl", 32, "bfloat16"), ("xh", 32, "bfloat16"),
+        ("scn", 32, "float32"), ("fl", 32, "bfloat16"), ("fo", 16, "uint16"),
         ("ya", 128, "bfloat16"), ("yb", 128, "bfloat16")):
     SCRATCH[_name] = ("sbuf", [128, _w], _t)
-for _name in ("p_l", "p_h", "p_f", "p_r0", "p_r1", "p_r2", "p_r3"):
+for _name in ("p_l", "p_h", "p_f", "p_g", "p_r0", "p_r1", "p_r2", "p_r3"):
     SCRATCH[_name] = ("psum", [128, 512], "float32")
-SEMAPHORES = ["v", "pe", "a", "gi", "dbp", "dst", "dtab", "dya", "dyb", "sa", "sb"] + ["m%d" % _m for _m in range(1, N)]
+SEMAPHORES = ["v", "pe", "a", "gi", "dbp", "dst", "dtab", "dya", "dyb", "sa"] + ["m%d" % _m for _m in range(1, N)]
 
 
 def land(T, m):
@@ -53,14 +52,14 @@ def plan(f, cores, topo):
     return straight, other, relay
 
 
-def send(g, src, dsts, f, T, topo, mask, local_sem):
+def send(g, src, dsts, f, T, topo, mask):
     ids = []
     for d in dsts:
         rid, pid = topo.addr(d, src)
         ids.append(DstId(rid=rid, pnc=pid))
     g.remote_dma_fused([RemoteDMATransfer(dst_ids=ids, dma_engine_mask=mask, remote_sem=T.sem["m%d" % f],
                                           srcs=[land(T, f)], dsts=[land(T, f) for d in dsts])],
-                       local_sem=local_sem)
+                       local_sem=T.sem.sa)
     return bits(mask)
 
 
@@ -78,7 +77,7 @@ def run_relay(g, core, f, other, T, topo):
         groups = pairs(other)
     n = 0
     for grp in groups:
-        n += send(g, core, [cores[d] for d in grp], f, T, topo, off, T.sem.sa)
+        n += send(g, core, [cores[d] for d in grp], f, T, topo, off)
     g.wait_ge(T.sem.sa, n)
 
 
@@ -108,12 +107,20 @@ def rank_program(g, core, T, topo):
     def vw(n):
         V.wait_ge(sem.v, n)
 
+    def mm(n_v, out, lhsT, rhs, start=True, stop=True):
+        if n_v:
+            PE.wait_ge(sem.v, n_v)
+        return done("pe", PE.matmul(out, lhsT, rhs, start, stop))
+
     if f > 0:
         g.sync.dma_start(T.raw[:, :], T.bp[:, :]).then_inc(sem.dbp, 16)
     if f == TOP:
+        g.sync.dma_start(T.wr[0:16, :], T.st[:, :]).then_inc(sem.dst, 16)
+    else:
         for k in range(8):
             q = A if k % 2 else g.sync
-            q.dma_start(T.wr[16 * k:16 * k + 16, :], T.st[:, 2 * k:2 * k + 2]).then_inc(sem.dst, 16)
+            q.dma_start(T.wr[16 * k:16 * k + 16, 0:2], T.st[:, 2 * k:2 * k + 2]).then_inc(sem.dst, 16)
+    g.sync.dma_start(T.tb[:, :], T.tab[:, :]).then_inc(sem.dtab, 16)
 
     done("gi", g.iota(T.pidx[:, :], [[0, 1]], 0, 1))
     done("gi", g.iota(T.pk[:, :], [[-1, 8]], 0, 1, allow_small_or_imprecise_dtypes=True))
@@ -121,42 +128,29 @@ def rank_program(g, core, T, topo):
     done("gi", g.iota(T.i_g[:, :], [[1, 8], [0, 16]], 0, 0, allow_small_or_imprecise_dtypes=True))
     V.wait_ge(sem.gi, 4)
     ts(T.pgr[:, 0:1], T.pidx[:, :], 4, None, Op.arith_shift_right)
-    ts(T.pgr[:, 1:2], T.pidx[:, :], 15, None, Op.bitwise_and)
+    n = ts(T.pgr[:, 1:2], T.pidx[:, :], 15, None, Op.bitwise_and)
     for k in range(8):
         n_rp = ts(T.rp[:, 128 * k:128 * k + 128], T.i_r[:, :], 8.0, T.pk[:, k:k + 1], Op.mult, Op.is_equal)
-    vw(n_rp)
+    vw(n)
     n_col = done("v", V.tensor_copy(T.col[:, :], T.pgr[:, :]))
 
-    n_prep = 0
+    n_sent = 0
     if f > 0:
         V.wait_ge(sem.dbp, 16)
         ts(T.sp[:, 0:64:2], T.raw[:, :], 3, 510, Op.arith_shift_right, Op.bitwise_and)
         n = ts(T.sp[:, 1:64:2], T.raw[:, :], 15, None, Op.bitwise_and)
         vw(n)
-        n_prep = done("v", V.tensor_copy(T.mp[:, :] if f == TOP else land(T, f), T.sp[:, :]))
-
-    state = {"sa": 0, "sb": 0}
-
-    def sends(ready):
-        for key, val in ready:
-            g.wait_ge(sem[key], val)
+        g.wait_ge(sem.v, done("v", V.tensor_copy(land(T, f), T.sp[:, :])))
         if relay is not None:
-            off = topo.mask(relay, cores[other[0]])
-            state["sa"] += send(g, core, [relay], f, T, topo, off, sem.sa)
-        for i, grp in enumerate(pairs(straight)):
-            key = "sa" if i == 0 else "sb"
-            state[key] += send(g, core, [cores[d] for d in grp], f, T, topo,
-                               topo.mask(core, cores[grp[0]]), sem[key])
-
-    if 0 < f < TOP:
-        sends([("v", n_prep)])
+            n_sent += send(g, core, [relay], f, T, topo, topo.mask(relay, cores[other[0]]))
+        for grp in pairs(straight):
+            n_sent += send(g, core, [cores[d] for d in grp], f, T, topo, topo.mask(core, cores[grp[0]]))
 
     pg, pr = T.col[:, 0:1], T.col[:, 1:2]
     i32 = T.i_r[:, 0:32]
     vw(n_col)
-    ts(T.bd[:, :], T.i_g[:, :], pg, None, Op.is_equal)
-    ts(T.bd8[:, :], T.i_g[:, :], pg, 8.0, Op.is_equal, Op.mult)
     ts(T.dg[:, :], i32, pr, None, Op.is_equal)
+    ts(T.bd[:, :], T.i_g[:, :], pg, None, Op.is_equal)
     n = ts(T.r1[:, :], pr, 1.0, None, Op.add)
     vw(n)
     ts(T.ct1[:, :], T.dg[:, :], -1.0, 1.0, Op.mult, Op.add)
@@ -165,145 +159,103 @@ def rank_program(g, core, T, topo):
     vw(n)
     done("v", V.tensor_tensor(T.ct[:, :], T.ct1[:, :], T.ct2[:, :], Op.add))
     ts(T.scl[:, :], T.sc1[:, :], 2.0 ** -14, None, Op.add)
-    ts(T.sd[:, :], i32, 0.0, None, Op.not_equal)
-    ts(T.gm[:, :], T.i_g[:, 0:128:16], pg, None, Op.is_equal)
-    n_const = ts(T.ex[:, :], T.i_r[:, :], pr, None, Op.is_equal)
+    ts(T.gs[:, :], T.i_g[:, 0:128:16], pg, None, Op.is_equal)
+    ts(T.ex[0:16, :], T.i_r[0:16, :], T.col[0:16, 1:2], None, Op.is_equal)
+    n_const = ts(T.ex8[0:16, :], T.i_r[0:16, :], T.col[0:16, 1:2], 8.0, Op.is_equal, Op.mult)
 
-    banks = {"next": 0}
-    bank_free = [0, 0, 0, 0]
-    wready = {}
-
-    def spread(m, src, waitsem, val):
-        PE.wait_ge(sem[waitsem], val)
-        n_a = 0
-        for h in range(2):
-            b = banks["next"]
-            banks["next"] = (b + 1) % 4
-            if bank_free[b]:
-                PE.wait_ge(sem.a, bank_free[b])
-            ps = T["p_r%d" % b]
-            n_pe = 0
-            for k in range(4):
-                kk = 4 * h + k
-                n_pe = done("pe", PE.matmul(ps[:, 64 * k:64 * k + 64], T.rp[:, 128 * kk:128 * kk + 128],
-                                            src, True, True))
-            A.wait_ge(sem.pe, n_pe)
-            n_a = done("a", A.activation(win(T, m, 256 * h, 256 * h + 256), ps[:, 0:256], Act.Copy))
-            bank_free[b] = n_a
-        wready[m] = n_a
-
-    turn = {"mk": 0}
-
-    def mask_of():
-        return T.mk[:, 32 * turn["mk"]:32 * turn["mk"] + 32]
-
-    def new_mask(lo_row):
-        turn["mk"] = 1 - turn["mk"]
-        return ts(mask_of(), lo_row, pr, None, Op.is_equal)
-
-    def gathers(m, n_state):
-        V.wait_ge(sem.a, wready[m])
-        vw(n_state)
-        o = T.offs[:, 0:2]
-        nl = done("v", V.tensor_tensor(T.xl[:, :], win(T, m, 1, 512).indirect(o), mask_of(), Op.mult))
-        nh = done("v", V.tensor_tensor(T.xh[:, :], win(T, m, 0, 511).indirect(o), mask_of(), Op.mult))
-        return nl, nh
-
-    def add_up(nl, nh):
-        PE.wait_ge(sem.v, nl)
-        a = done("pe", PE.matmul(T.p_l[:, 0:32], T.bd[:, :], T.xl[:, :], True, True))
-        PE.wait_ge(sem.v, nh)
-        b = done("pe", PE.matmul(T.p_h[:, 0:32], T.bd[:, :], T.xh[:, :], True, True))
-        return a, b
-
-    def next_state(lo_row, hi_row, nl=0, nh=0):
-        if nl:
-            V.wait_ge(sem.pe, nl)
-        new_mask(lo_row)
-        if nh:
-            V.wait_ge(sem.pe, nh)
-        n1 = done("v", V.tensor_tensor_scan(T.scn[:, :], T.ct[:, :], hi_row, 0.0, Op.mult, Op.add))
-        vw(n1)
-        return ts(T.offs[:, :], T.scn[:, 15:32:16], T.scl[:, :], None, Op.mult)
-
-    hi_pay = T.land[:, 64 * TOP:64 * TOP + 32]
-    lo_pay = T.land[:, 64 * TOP + 32:64 * TOP + 64]
     if f == TOP:
-        V.wait_ge(sem.dst, 128)
-        ts(T.wsp[:, 0:2], T.wr[:, :], 3, 510, Op.arith_shift_right, Op.bitwise_and)
-        n = ts(T.wsp[:, 2:4], T.wr[:, :], 15, None, Op.bitwise_and)
+        V.wait_ge(sem.dst, 16)
+        ts(T.wsp[0:16, 0:16], T.wr[0:16, :], 3, 510, Op.arith_shift_right, Op.bitwise_and)
+        n = ts(T.wsp[0:16, 16:32], T.wr[0:16, :], 15, None, Op.bitwise_and)
         vw(n)
-        done("v", V.tensor_copy(T.lof[:, :], T.wsp[:, 2:4]))
-        n = done("v", V.tensor_copy(T.offs[:, :], T.wsp[:, 0:2]))
+        n_fl = done("v", V.tensor_copy(T.fl[0:16, :], T.wsp[0:16, :]))
+    else:
+        V.wait_ge(sem.dst, 128)
+        ts(T.wsp[:, 0:2], T.wr[:, 0:2], 3, 510, Op.arith_shift_right, Op.bitwise_and)
+        n = ts(T.wsp[:, 2:4], T.wr[:, 0:2], 15, None, Op.bitwise_and)
+        vw(n)
+        done("v", V.tensor_copy(T.offs[:, :], T.wsp[:, 0:2]))
+        n = done("v", V.tensor_copy(T.lof[:, :], T.wsp[:, 2:4]))
         vw(n)
         ts(T.rl[:, 0:16], T.dg[:, 0:16], T.lof[:, 0:1], None, Op.mult)
-        n_rl = ts(T.rl[:, 16:32], T.dg[:, 16:32], T.lof[:, 1:2], None, Op.mult)
-        spread(TOP, T.mp[:, :], "v", n_prep)
-        PE.wait_ge(sem.v, n_rl)
-        n_l = done("pe", PE.matmul(T.p_l[:, 0:32], T.bd[:, :], T.rl[:, :], True, True))
-        V.wait_ge(sem.pe, n_l)
-        n = new_mask(T.p_l[:, 0:32])
-        nl, nh = gathers(TOP, n)
-        a, b = add_up(nl, nh)
-        V.wait_ge(sem.pe, a)
-        n_v = done("v", V.tensor_copy(lo_pay, T.p_l[:, 0:32]))
-        A.wait_ge(sem.pe, b)
-        n_a = done("a", A.activation(hi_pay, T.p_h[:, 0:32], Act.Copy))
-        sends([("v", n_v), ("a", n_a)])
-        n_s2 = done("v", V.tensor_copy(T.s2[:, 15:32:16], T.wr[:, :]))
-    else:
+        n = ts(T.rl[:, 16:32], T.dg[:, 16:32], T.lof[:, 1:2], None, Op.mult)
+        V.wait_ge(sem.pe, mm(n, T.p_l[:, 0:32], T.bd[:, :], T.rl[:, :]))
+        n_state = ts(T.mk[:, :], T.p_l[:, 0:32], pr, None, Op.is_equal)
+
         arrived = bits(topo.mask(cores[TOP], cores[0]))
-        if f < TOP - 1:
-            maps = list(range(TOP - 1, f, -1))
-            late = [m for m in maps if not topo.may_write(cores[m], core)]
-            PE.wait_ge(sem.v, n_rp)
-            for m in maps:
-                if m not in late:
-                    spread(m, land(T, m), "m%d" % m, arrived)
-            V.wait_ge(sem["m%d" % TOP], arrived)
-            vw(n_const)
-            n_state = next_state(lo_pay, hi_pay)
-            nl = nh = 0
-            for m in maps:
-                while m not in wready:
-                    x = late.pop(0)
-                    spread(x, land(T, x), "m%d" % x, arrived)
-                nl, nh = gathers(m, n_state)
-                if m > f + 1:
-                    a, b = add_up(nl, nh)
-                    n_state = next_state(T.p_l[:, 0:32], T.p_h[:, 0:32], a, b)
-                    if late:
-                        x = late.pop(0)
-                        spread(x, land(T, x), "m%d" % x, arrived)
-            PE.wait_ge(sem.v, nl)
-            done("pe", PE.matmul(T.p_f[:, 0:32], T.bd[:, :], T.xl[:, :], True, False))
-            PE.wait_ge(sem.v, nh)
-            n = done("pe", PE.matmul(T.p_f[:, 0:32], T.bd8[:, :], T.xh[:, :], False, True))
-            V.wait_ge(sem.pe, n)
-            row = T.p_f[:, 0:32]
-        else:
-            V.wait_ge(sem["m%d" % TOP], arrived)
-            vw(n_const)
-            n = ts(T.ys[:, :], hi_pay, 8.0, None, Op.mult)
-            vw(n)
-            n = done("v", V.tensor_tensor(T.z[:, :], T.ys[:, :], lo_pay, Op.add))
-            vw(n)
-            row = T.z[:, :]
-        n = done("v", V.tensor_tensor(T.ys[:, :], row, T.dg[:, :], Op.mult))
-        vw(n)
-        n_s2 = done("v", V.tensor_tensor_scan(T.s2[:, :], T.sd[:, :], T.ys[:, :], 0.0, Op.mult, Op.add))
+        banks = {"next": 0}
+        bank_free = [("a", 0)] * 4
+        wready = {}
 
-    vw(n_s2)
-    ts(T.rr[:, 0:16:2], T.gm[:, :], T.s2[:, 15:16], None, Op.mult)
-    n = ts(T.rr[:, 1:16:2], T.gm[:, :], T.s2[:, 31:32], None, Op.mult)
-    PE.wait_ge(sem.v, n)
-    n = done("pe", PE.matmul(T.p_f[:, 0:16], T.ex[:, :], T.rr[:, :], True, True))
+        def spread(m, parts, both):
+            PE.wait_ge(sem["m%d" % m], arrived)
+            ready = {}
+            per = 8 // parts
+            w = 64 * per
+            for h in range(parts):
+                b = banks["next"]
+                banks["next"] = (b + 1) % 4
+                key, val = bank_free[b]
+                if val:
+                    PE.wait_ge(sem[key], val)
+                ps = T["p_r%d" % b]
+                n_pe = 0
+                for k in range(per):
+                    kk = per * h + k
+                    n_pe = mm(0, ps[:, 64 * k:64 * k + 64], T.rp[:, 128 * kk:128 * kk + 128], land(T, m))
+                dst = win(T, m, w * h, w * h + w)
+                if both and h % 2:
+                    V.wait_ge(sem.pe, n_pe)
+                    bank_free[b] = ("v", done("v", V.tensor_copy(dst, ps[:, 0:w])))
+                else:
+                    A.wait_ge(sem.pe, n_pe)
+                    bank_free[b] = ("a", done("a", A.activation(dst, ps[:, 0:w], Act.Copy)))
+                ready[bank_free[b][0]] = bank_free[b][1]
+            wready[m] = ready
+
+        maps = list(range(TOP, f, -1))
+        late = [m for m in maps if not topo.may_write(cores[m], core)]
+        first_late = late[0] if late else None
+
+        def spread_late():
+            x = late.pop(0)
+            spread(x, 4 if x == first_late else 2, x == first_late)
+
+        for m in maps:
+            if m not in late:
+                spread(m, 2, False)
+        nh = nl = 0
+        for m in maps:
+            while m not in wready:
+                spread_late()
+            for key in wready[m]:
+                V.wait_ge(sem[key], wready[m][key])
+            vw(n_state)
+            o = T.offs[:, 0:2]
+            nh = done("v", V.tensor_tensor(T.xh[:, :], win(T, m, 0, 511).indirect(o), T.mk[:, :], Op.mult))
+            nl = done("v", V.tensor_tensor(T.xl[:, :], win(T, m, 1, 512).indirect(o), T.mk[:, :], Op.mult))
+            if m > f + 1:
+                h = mm(nh, T.p_h[:, 0:32], T.bd[:, :], T.xh[:, :])
+                l = mm(nl, T.p_l[:, 0:32], T.bd[:, :], T.xl[:, :])
+                V.wait_ge(sem.pe, h)
+                n = done("v", V.tensor_tensor_scan(T.scn[:, :], T.ct[:, :], T.p_h[:, 0:32], 0.0, Op.mult, Op.add))
+                V.wait_ge(sem.pe, l)
+                ts(T.mk[:, :], T.p_l[:, 0:32], pr, None, Op.is_equal)
+                vw(n)
+                n_state = ts(T.offs[:, :], T.scn[:, 15:32:16], T.scl[:, :], None, Op.mult)
+                if late:
+                    spread_late()
+        for c in range(2):
+            mm(nh if c == 0 else 0, T.p_f[0:16, c:16:2], T.xh[:, 16 * c:16 * c + 16], T.gs[:, :])
+        for c in range(2):
+            n = mm(nl if c == 0 else 0, T.p_f[0:16, 16 + c:32:2], T.xl[:, 16 * c:16 * c + 16], T.gs[:, :])
+        V.wait_ge(sem.pe, n)
+        n_fl = done("v", V.tensor_copy(T.fl[0:16, :], T.p_f[0:16, 0:32]))
+
+    mm(n_fl, T.p_g[:, 0:16], T.ex8[0:16, :], T.fl[0:16, 0:16], True, False)
+    n = mm(0, T.p_g[:, 0:16], T.ex[0:16, :], T.fl[0:16, 16:32], False, True)
     V.wait_ge(sem.pe, n)
-    n_fo = done("v", V.tensor_copy(T.fo[:, :], T.p_f[:, 0:16]))
-
-    if state["sa"]:
-        g.sync.wait_ge(sem.sa, state["sa"])
-    g.sync.dma_start(T.tb[:, :], T.tab[:, :]).then_inc(sem.dtab, 16)
+    n_fo = done("v", V.tensor_copy(T.fo[:, :], T.p_g[:, 0:16]))
 
     V.wait_ge(sem.dtab, 16)
     vw(n_fo)
@@ -317,10 +269,8 @@ def rank_program(g, core, T, topo):
     A.dma_start(T.y[:, 128:256], T.yb[:, :]).then_inc(sem.dyb, 16)
 
     for key in ("v", "pe", "a"):
-        if cnt[key]:
-            g.wait_ge(sem[key], cnt[key])
-    for key in ("sa", "sb"):
-        if state[key]:
-            g.wait_ge(sem[key], state[key])
+        g.wait_ge(sem[key], cnt[key])
+    if n_sent:
+        g.wait_ge(sem.sa, n_sent)
     g.wait_ge(sem.dya, 16)
     g.wait_ge(sem.dyb, 16)

@@ -126,13 +126,6 @@ def rank_program(g, core, T, topo):
     done("gi", g.iota(T.pk[:, :], [[-1, 8]], 0, 1, allow_small_or_imprecise_dtypes=True))
     done("gi", g.iota(T.i_r[:, :], [[0, 8], [1, 16]], 0, 0, allow_small_or_imprecise_dtypes=True))
     done("gi", g.iota(T.i_g[:, :], [[1, 8], [0, 16]], 0, 0, allow_small_or_imprecise_dtypes=True))
-    V.wait_ge(sem.gi, 4)
-    ts(T.pgr[:, 0:1], T.pidx[:, :], 4, None, Op.arith_shift_right)
-    n = ts(T.pgr[:, 1:2], T.pidx[:, :], 15, None, Op.bitwise_and)
-    for k in range(8):
-        n_rp = ts(T.rp[:, 128 * k:128 * k + 128], T.i_r[:, :], 8.0, T.pk[:, k:k + 1], Op.mult, Op.is_equal)
-    vw(n)
-    n_col = done("v", V.tensor_copy(T.col[:, :], T.pgr[:, :]))
 
     n_sent = 0
     if f > 0:
@@ -146,29 +139,22 @@ def rank_program(g, core, T, topo):
         for grp in pairs(straight):
             n_sent += send(g, core, [cores[d] for d in grp], f, T, topo, topo.mask(core, cores[grp[0]]))
 
+    V.wait_ge(sem.gi, 4)
+    ts(T.pgr[:, 0:1], T.pidx[:, :], 4, None, Op.arith_shift_right)
+    n = ts(T.pgr[:, 1:2], T.pidx[:, :], 15, None, Op.bitwise_and)
+    vw(n)
+    n_col = done("v", V.tensor_copy(T.col[:, :], T.pgr[:, :]))
     pg, pr = T.col[:, 0:1], T.col[:, 1:2]
     i32 = T.i_r[:, 0:32]
     vw(n_col)
     ts(T.dg[:, :], i32, pr, None, Op.is_equal)
-    ts(T.bd[:, :], T.i_g[:, :], pg, None, Op.is_equal)
-    n = ts(T.r1[:, :], pr, 1.0, None, Op.add)
-    vw(n)
-    ts(T.ct1[:, :], T.dg[:, :], -1.0, 1.0, Op.mult, Op.add)
-    ts(T.sc1[:, :], pr, 15.0, 1.0 - 2.0 ** -14, Op.is_equal, Op.mult)
-    n = ts(T.ct2[:, :], i32, T.r1[:, :], 16383.0, Op.is_equal, Op.mult)
-    vw(n)
-    done("v", V.tensor_tensor(T.ct[:, :], T.ct1[:, :], T.ct2[:, :], Op.add))
-    ts(T.scl[:, :], T.sc1[:, :], 2.0 ** -14, None, Op.add)
-    ts(T.gs[:, :], T.i_g[:, 0:128:16], pg, None, Op.is_equal)
-    ts(T.ex[0:16, :], T.i_r[0:16, :], T.col[0:16, 1:2], None, Op.is_equal)
-    n_const = ts(T.ex8[0:16, :], T.i_r[0:16, :], T.col[0:16, 1:2], 8.0, Op.is_equal, Op.mult)
-
+    n_bd = ts(T.bd[:, :], T.i_g[:, :], pg, None, Op.is_equal)
     if f == TOP:
         V.wait_ge(sem.dst, 16)
         ts(T.wsp[0:16, 0:16], T.wr[0:16, :], 3, 510, Op.arith_shift_right, Op.bitwise_and)
         n = ts(T.wsp[0:16, 16:32], T.wr[0:16, :], 15, None, Op.bitwise_and)
         vw(n)
-        n_fl = done("v", V.tensor_copy(T.fl[0:16, :], T.wsp[0:16, :]))
+        done("v", V.tensor_copy(T.fl[0:16, :], T.wsp[0:16, :]))
     else:
         V.wait_ge(sem.dst, 128)
         ts(T.wsp[:, 0:2], T.wr[:, 0:2], 3, 510, Op.arith_shift_right, Op.bitwise_and)
@@ -179,9 +165,24 @@ def rank_program(g, core, T, topo):
         vw(n)
         ts(T.rl[:, 0:16], T.dg[:, 0:16], T.lof[:, 0:1], None, Op.mult)
         n = ts(T.rl[:, 16:32], T.dg[:, 16:32], T.lof[:, 1:2], None, Op.mult)
-        V.wait_ge(sem.pe, mm(n, T.p_l[:, 0:32], T.bd[:, :], T.rl[:, :]))
+        n_rl = mm(n, T.p_l[:, 0:32], T.bd[:, :], T.rl[:, :])
+        for k in range(8):
+            n_rp = ts(T.rp[:, 128 * k:128 * k + 128], T.i_r[:, :], 8.0, T.pk[:, k:k + 1], Op.mult, Op.is_equal)
+        V.wait_ge(sem.pe, n_rl)
         n_state = ts(T.mk[:, :], T.p_l[:, 0:32], pr, None, Op.is_equal)
+        n = ts(T.r1[:, :], pr, 1.0, None, Op.add)
+        vw(n)
+        ts(T.ct1[:, :], T.dg[:, :], -1.0, 1.0, Op.mult, Op.add)
+        ts(T.sc1[:, :], pr, 15.0, 1.0 - 2.0 ** -14, Op.is_equal, Op.mult)
+        n = ts(T.ct2[:, :], i32, T.r1[:, :], 16383.0, Op.is_equal, Op.mult)
+        vw(n)
+        done("v", V.tensor_tensor(T.ct[:, :], T.ct1[:, :], T.ct2[:, :], Op.add))
+        ts(T.scl[:, :], T.sc1[:, :], 2.0 ** -14, None, Op.add)
+        n_state = ts(T.gs[:, :], T.i_g[:, 0:128:16], pg, None, Op.is_equal)
+    ts(T.ex[0:16, :], T.i_r[0:16, :], T.col[0:16, 1:2], None, Op.is_equal)
+    n_fl = ts(T.ex8[0:16, :], T.i_r[0:16, :], T.col[0:16, 1:2], 8.0, Op.is_equal, Op.mult)
 
+    if f != TOP:
         arrived = bits(topo.mask(cores[TOP], cores[0]))
         banks = {"next": 0}
         bank_free = [("a", 0)] * 4
@@ -221,12 +222,15 @@ def rank_program(g, core, T, topo):
             x = late.pop(0)
             spread(x, 4 if x == first_late else 2, x == first_late)
 
+        PE.wait_ge(sem.v, n_rp)
         for m in maps:
             if m not in late:
                 spread(m, 2, False)
         nh = nl = 0
         for m in maps:
             while m not in wready:
+                spread_late()
+            if m == first_late and late and late[0] == m - 1:
                 spread_late()
             for key in wready[m]:
                 V.wait_ge(sem[key], wready[m][key])

@@ -3,25 +3,33 @@ from concourse.mybir import AluOpType as Op, ActivationFunctionType as Act
 
 N = 12
 TOP = N - 1
+TEAMS = (((5, 4), (0, 1, 2, 3), 4), ((3, 2), (0, 1), 4))
+SLOTS = N + len(TEAMS)
+EARLY = 4
 SCRATCH = {
-    "land": ("sbuf", [128, 64 * N], "bfloat16"),
-    "win": ("sbuf", [128, 512 * N], "bfloat16"),
+    "land": ("sbuf", [128, 64 * SLOTS], "bfloat16"),
+    "win": ("sbuf", [128, 512 * SLOTS], "bfloat16"),
     "tb": ("sbuf", [128, 4096], "bfloat16"),
 }
 for _name, _w, _t in (
-        ("raw", 32, "int32"), ("sp", 64, "int32"), ("pidx", 1, "int32"), ("pgr", 2, "int32"),
-        ("col", 2, "float32"), ("pk", 8, "float32"), ("i_r", 128, "bfloat16"), ("i_g", 128, "bfloat16"),
-        ("rp", 1024, "bfloat16"), ("bd", 128, "bfloat16"), ("ex", 128, "bfloat16"), ("ex8", 128, "bfloat16"),
-        ("dg", 32, "bfloat16"), ("ct1", 32, "float32"), ("ct2", 32, "float32"), ("ct", 32, "float32"),
+        ("raw", 32, "int32"), ("sp", 64, "int32"), ("pidx", 1, "int32"), ("pgr", 5, "int32"),
+        ("col", 5, "float32"), ("mi", 128, "int32"), ("mr", 128, "int32"), ("mg", 128, "int32"),
+        ("cof", 8, "uint16"), ("coi", 8, "int32"), ("df", 128, "bfloat16"), ("dfc", 128, "bfloat16"),
+        ("i_r", 128, "bfloat16"), ("i_g", 128, "bfloat16"),
+        ("rp", 1024, "bfloat16"), ("rpc", 1024, "bfloat16"), ("reord", 128, "bfloat16"),
+        ("bd", 128, "bfloat16"), ("bdx", 128, "bfloat16"), ("ex", 128, "bfloat16"), ("ex8", 128, "bfloat16"),
+        ("dg", 128, "bfloat16"), ("dgx", 128, "bfloat16"), ("ct1", 128, "float32"), ("ct2", 128, "float32"),
+        ("ct", 256, "float32"),
         ("r1", 1, "float32"), ("sc1", 1, "float32"), ("scl", 1, "float32"), ("gs", 8, "bfloat16"),
-        ("wr", 16, "int32"), ("wsp", 32, "int32"), ("lof", 2, "float32"), ("rl", 32, "bfloat16"),
-        ("offs", 2, "uint16"), ("mk", 32, "bfloat16"), ("xl", 32, "bfloat16"), ("xh", 32, "bfloat16"),
-        ("scn", 32, "float32"), ("fl", 32, "bfloat16"), ("fo", 16, "uint16"),
+        ("wr", 16, "int32"), ("wsp", 32, "int32"), ("lof", 2, "float32"), ("rl", 128, "bfloat16"),
+        ("offs", 8, "uint16"), ("mk", 128, "bfloat16"), ("xl", 128, "bfloat16"), ("xh", 128, "bfloat16"),
+        ("scn", 256, "float32"), ("fl", 32, "bfloat16"), ("fo", 16, "uint16"),
+        ("emu", 16, "uint16"), ("em", 16, "bfloat16"),
         ("ya", 128, "bfloat16"), ("yb", 128, "bfloat16")):
     SCRATCH[_name] = ("sbuf", [128, _w], _t)
 for _name in ("p_l", "p_h", "p_f", "p_g", "p_r0", "p_r1", "p_r2", "p_r3"):
     SCRATCH[_name] = ("psum", [128, 512], "float32")
-SEMAPHORES = ["v", "pe", "a", "gi", "dbp", "dst", "dtab", "dya", "dyb", "sa"] + ["m%d" % _m for _m in range(1, N)]
+SEMAPHORES = ["v", "pe", "a", "gi", "dbp", "dst", "dtab", "dya", "dyb", "sa"] + ["m%d" % _m for _m in range(1, SLOTS)]
 
 
 def land(T, m):
@@ -36,20 +44,54 @@ def bits(mask):
     return bin(mask).count("1")
 
 
-def relay_of(src, dsts, topo, ncores):
-    for c in range(ncores):
-        if c != src and topo.host(c) == topo.host(src) and topo.chip(c) == topo.chip(src) \
-                and topo.die(c) == topo.die(src) and all(topo.may_write(c, d) for d in dsts):
-            return c
-    raise ValueError("no relay")
+def place(topo, c):
+    return topo.host(c), topo.chip(c)
 
 
-def plan(f, cores, topo):
+def team_cores(cores, topo):
+    taken = set(place(topo, c) for c in cores)
+    used, out = set(), []
+    for t, (maps, ranks, n) in enumerate(TEAMS):
+        fits = [c for c in range(256) if place(topo, c) not in taken and c not in used
+                and topo.die(c) == topo.die(cores[0]) and topo.same_plane(cores[maps[0]], c)
+                and all(topo.may_write(c, cores[r]) for r in ranks)]
+        team, seen = [], set()
+        for c in (fits if t % 2 == 0 else fits[::-1]):
+            if place(topo, c) not in seen and len(team) < n:
+                team.append(c)
+                seen.add(place(topo, c))
+        if len(team) < n:
+            raise ValueError("no team")
+        used |= set(team)
+        out.append(team)
+    return out
+
+
+def chain(f):
+    out = list(range(TOP, f, -1))
+    for t, (maps, ranks, n) in enumerate(TEAMS):
+        if f in ranks:
+            i = out.index(maps[0])
+            out[i:i + len(maps)] = [N + t]
+    return out
+
+
+def receivers(f, cores, topo, teams):
     src = cores[f]
-    straight = [d for d in range(f) if topo.may_write(src, cores[d])]
-    other = [d for d in range(f) if not topo.may_write(src, cores[d])]
-    relay = relay_of(src, [cores[d] for d in other], topo, 256) if other else None
-    return straight, other, relay
+    ok = topo.may_write
+    ranks = [cores[d] for d in range(f) if f in chain(d)]
+    helpers = [teams[t] for t in range(len(TEAMS)) if f in TEAMS[t][0]]
+    near_ranks = [d for d in ranks if ok(src, d)]
+    straight = [[d for d in team if ok(src, d)] for team in helpers]
+    straight += [near_ranks[i:i + 2] for i in range(0, len(near_ranks), 2)]
+    straight = [grp for grp in straight if grp]
+    far = [d for d in ranks if not ok(src, d)] + [d for team in helpers for d in team if not ok(src, d)]
+    relay, groups = None, []
+    if far:
+        relay = [c for c in range(256) if c != src and place(topo, c) == place(topo, src)
+                 and topo.die(c) == topo.die(src) and all(ok(c, d) for d in far)][0]
+        groups = [[d] for d in far[:2]] + [far[i:i + 2] for i in range(2, len(far), 2)]
+    return straight, relay, groups
 
 
 def send(g, src, dsts, f, T, topo, mask):
@@ -63,38 +105,37 @@ def send(g, src, dsts, f, T, topo, mask):
     return bits(mask)
 
 
-def pairs(lst):
-    return [lst[i:i + 2] for i in range(0, len(lst), 2)]
-
-
-def run_relay(g, core, f, other, T, topo):
-    cores = list(T.cores)
-    off = topo.mask(core, cores[other[0]])
+def run_relay(g, core, f, groups, T, topo):
+    off = topo.mask(core, groups[0][0])
     g.wait_ge(T.sem["m%d" % f], bits(off))
-    if 0 in other:
-        groups = [[d] for d in other[:2]] + pairs(other[2:])
-    else:
-        groups = pairs(other)
     n = 0
     for grp in groups:
-        n += send(g, core, [cores[d] for d in grp], f, T, topo, off)
+        n += send(g, core, grp, f, T, topo, off)
     g.wait_ge(T.sem.sa, n)
 
 
 def rank_program(g, core, T, topo):
     cores = list(T.cores)
     f = T.rank_of(core)
-    if f is None:
-        for r in range(1, N):
-            straight, other, relay = plan(r, cores, topo)
-            if relay == core:
-                run_relay(g, core, r, other, T, topo)
-        return
+    teams = team_cores(cores, topo)
+    is_rank = f is not None
+    team = part = None
+    if not is_rank:
+        for t in range(len(TEAMS)):
+            if core in teams[t]:
+                team, part = t, teams[t].index(core)
+        if team is None:
+            for r in range(1, N):
+                straight, relay, groups = receivers(r, cores, topo, teams)
+                if relay == core:
+                    run_relay(g, core, r, groups, T, topo)
+            return
 
     sem = T.sem
-    straight, other, relay = plan(f, cores, topo)
     cnt = {"v": 0, "pe": 0, "a": 0, "gi": 0}
     V, PE, A = g.vector, g.tensor, g.scalar
+    off_mask = topo.mask(cores[TOP], cores[0])
+    arrived = bits(off_mask)
 
     def done(key, ins):
         ins.then_inc(sem[key], 1)
@@ -104,6 +145,9 @@ def rank_program(g, core, T, topo):
     def ts(out, in0, s1, s2, *ops):
         return done("v", V.tensor_scalar(out, in0, s1, s2, *ops))
 
+    def copy(out, in_):
+        return done("v", V.tensor_copy(out, in_))
+
     def vw(n):
         V.wait_ge(sem.v, n)
 
@@ -112,87 +156,135 @@ def rank_program(g, core, T, topo):
             PE.wait_ge(sem.v, n_v)
         return done("pe", PE.matmul(out, lhsT, rhs, start, stop))
 
-    if f > 0:
-        g.sync.dma_start(T.raw[:, :], T.bp[:, :]).then_inc(sem.dbp, 16)
-    if f == TOP:
-        g.sync.dma_start(T.wr[0:16, :], T.st[:, :]).then_inc(sem.dst, 16)
-    else:
-        for k in range(8):
-            q = A if k % 2 else g.sync
-            q.dma_start(T.wr[16 * k:16 * k + 16, 0:2], T.st[:, 2 * k:2 * k + 2]).then_inc(sem.dst, 16)
-    g.sync.dma_start(T.tb[:, :], T.tab[:, :]).then_inc(sem.dtab, 16)
+    maps = chain(f) if is_rank else list(TEAMS[team][0][1:])
+    comps = [m for m in maps if m >= N]
+    nc = 2 if is_rank else 32 // TEAMS[team][2]
+    w = 16 * nc
+
+    if is_rank:
+        if f > 0:
+            g.sync.dma_start(T.raw[:, :], T.bp[:, :]).then_inc(sem.dbp, 16)
+        if f == TOP:
+            g.sync.dma_start(T.wr[0:16, :], T.st[:, :]).then_inc(sem.dst, 16)
+        else:
+            for k in range(8):
+                q = A if k % 2 else g.sync
+                q.dma_start(T.wr[16 * k:16 * k + 16, 0:2], T.st[:, 2 * k:2 * k + 2]).then_inc(sem.dst, 16)
+        g.sync.dma_start(T.tb[:, :], T.tab[:, :]).then_inc(sem.dtab, 16)
 
     done("gi", g.iota(T.pidx[:, :], [[0, 1]], 0, 1))
-    done("gi", g.iota(T.pk[:, :], [[-1, 8]], 0, 1, allow_small_or_imprecise_dtypes=True))
-    done("gi", g.iota(T.i_r[:, :], [[0, 8], [1, 16]], 0, 0, allow_small_or_imprecise_dtypes=True))
-    done("gi", g.iota(T.i_g[:, :], [[1, 8], [0, 16]], 0, 0, allow_small_or_imprecise_dtypes=True))
+    done("gi", g.iota(T.mi[:, :], [[1, 128]], 0, 0))
+    if not is_rank:
+        done("gi", g.iota(T.coi[:, 0:nc], [[2, nc]], 1, 0))
 
     n_sent = 0
-    if f > 0:
+    if is_rank and f > 0:
+        straight, relay, groups = receivers(f, cores, topo, teams)
         V.wait_ge(sem.dbp, 16)
         ts(T.sp[:, 0:64:2], T.raw[:, :], 3, 510, Op.arith_shift_right, Op.bitwise_and)
         n = ts(T.sp[:, 1:64:2], T.raw[:, :], 15, None, Op.bitwise_and)
         vw(n)
-        g.wait_ge(sem.v, done("v", V.tensor_copy(land(T, f), T.sp[:, :])))
-        if relay is not None:
-            n_sent += send(g, core, [relay], f, T, topo, topo.mask(relay, cores[other[0]]))
-        for grp in pairs(straight):
-            n_sent += send(g, core, [cores[d] for d in grp], f, T, topo, topo.mask(core, cores[grp[0]]))
+        g.wait_ge(sem.v, copy(land(T, f), T.sp[:, :]))
+        if groups:
+            n_sent += send(g, core, [relay], f, T, topo, off_mask)
+        for grp in straight:
+            n_sent += send(g, core, grp, f, T, topo, topo.mask(core, grp[0]))
 
-    V.wait_ge(sem.gi, 4)
+    V.wait_ge(sem.gi, cnt["gi"])
     ts(T.pgr[:, 0:1], T.pidx[:, :], 4, None, Op.arith_shift_right)
-    n = ts(T.pgr[:, 1:2], T.pidx[:, :], 15, None, Op.bitwise_and)
+    ts(T.pgr[:, 1:2], T.pidx[:, :], 15, None, Op.bitwise_and)
+    ts(T.mr[:, :], T.mi[:, :], 15, None, Op.bitwise_and)
+    ts(T.mg[:, :], T.mi[:, :], 4, None, Op.arith_shift_right)
+    npg = 3
+    if not is_rank:
+        npg = 5
+        ts(T.pgr[:, 3:4], T.pidx[:, :], 3, None, Op.arith_shift_right)
+        ts(T.pgr[:, 4:5], T.pidx[:, :], 7, None, Op.bitwise_and)
+    n = copy(T.pgr[:, 2:3], T.pidx[:, :])
     vw(n)
-    n_col = done("v", V.tensor_copy(T.col[:, :], T.pgr[:, :]))
-    pg, pr = T.col[:, 0:1], T.col[:, 1:2]
-    i32 = T.i_r[:, 0:32]
+    copy(T.i_r[:, :], T.mr[:, :])
+    copy(T.i_g[:, :], T.mg[:, :])
+    n_col = copy(T.col[:, 0:npg], T.pgr[:, 0:npg])
+    pg, pr, pp = T.col[:, 0:1], T.col[:, 1:2], T.col[:, 2:3]
+    iw = T.i_r[:, 0:w]
     vw(n_col)
-    ts(T.dg[:, :], i32, pr, None, Op.is_equal)
-    n_bd = ts(T.bd[:, :], T.i_g[:, :], pg, None, Op.is_equal)
-    if f == TOP:
+    ts(T.dg[:, 0:w], iw, pr, None, Op.is_equal)
+    n_df = ts(T.df[:, :], T.i_r[:, :], 8.0, pp, Op.mult, Op.subtract)
+    ts(T.bd[:, :], T.i_g[:, :], pg, None, Op.is_equal)
+
+    def spread_consts():
+        vw(n_df)
+        for k in range(8):
+            n = ts(T.rp[:, 128 * k:128 * k + 128], T.df[:, :], -float(k), None, Op.is_equal)
+        return n
+
+    def scan_consts():
+        n = ts(T.r1[:, :], pr, 1.0, None, Op.add)
+        vw(n)
+        ts(T.ct1[:, 0:w], T.dg[:, 0:w], -1.0, 1.0, Op.mult, Op.add)
+        ts(T.sc1[:, :], pr, 15.0, 1.0 - 2.0 ** -14, Op.is_equal, Op.mult)
+        n = ts(T.ct2[:, 0:w], iw, T.r1[:, :], 16383.0, Op.is_equal, Op.mult)
+        vw(n)
+        done("v", V.tensor_tensor(T.ct[:, 0:w], T.ct1[:, 0:w], T.ct2[:, 0:w], Op.add))
+        if not is_rank:
+            done("v", V.tensor_tensor(T.ct[:, w:2 * w], T.ct1[:, 0:w], T.ct2[:, 0:w], Op.add))
+        return ts(T.scl[:, :], T.sc1[:, :], 2.0 ** -14, None, Op.add)
+
+    n_rp = n_rpc = n_reord = n_state = n_fl = 0
+    if not is_rank:
+        copy(T.cof[:, 0:nc], T.coi[:, 0:nc])
+        ts(T.dgx[:, 0:w], iw, T.col[:, 3:4], None, Op.is_equal)
+        ts(T.bdx[:, :], T.i_g[:, :], T.col[:, 4:5], None, Op.is_equal)
+        vw(n_df)
+        n = done("v", V.tensor_tensor(T.ct1[:, 0:128], T.df[:, :], T.i_g[:, :], Op.add))
+        vw(n)
+        n_reord = ts(T.reord[:, :], T.ct1[:, 0:128], 0.0, None, Op.is_equal)
+        n_rp = spread_consts()
+        n_state = scan_consts()
+    elif f == TOP:
         V.wait_ge(sem.dst, 16)
         ts(T.wsp[0:16, 0:16], T.wr[0:16, :], 3, 510, Op.arith_shift_right, Op.bitwise_and)
         n = ts(T.wsp[0:16, 16:32], T.wr[0:16, :], 15, None, Op.bitwise_and)
         vw(n)
-        done("v", V.tensor_copy(T.fl[0:16, :], T.wsp[0:16, :]))
+        copy(T.fl[0:16, :], T.wsp[0:16, :])
     else:
         V.wait_ge(sem.dst, 128)
         ts(T.wsp[:, 0:2], T.wr[:, 0:2], 3, 510, Op.arith_shift_right, Op.bitwise_and)
         n = ts(T.wsp[:, 2:4], T.wr[:, 0:2], 15, None, Op.bitwise_and)
         vw(n)
-        done("v", V.tensor_copy(T.offs[:, :], T.wsp[:, 0:2]))
-        n = done("v", V.tensor_copy(T.lof[:, :], T.wsp[:, 2:4]))
+        copy(T.offs[:, 0:2], T.wsp[:, 0:2])
+        n = copy(T.lof[:, :], T.wsp[:, 2:4])
         vw(n)
         ts(T.rl[:, 0:16], T.dg[:, 0:16], T.lof[:, 0:1], None, Op.mult)
         n = ts(T.rl[:, 16:32], T.dg[:, 16:32], T.lof[:, 1:2], None, Op.mult)
-        n_rl = mm(n, T.p_l[:, 0:32], T.bd[:, :], T.rl[:, :])
-        for k in range(8):
-            n_rp = ts(T.rp[:, 128 * k:128 * k + 128], T.i_r[:, :], 8.0, T.pk[:, k:k + 1], Op.mult, Op.is_equal)
+        n_rl = mm(n, T.p_l[:, 0:32], T.bd[:, :], T.rl[:, 0:32])
+        n_rp = spread_consts()
         V.wait_ge(sem.pe, n_rl)
-        n_state = ts(T.mk[:, :], T.p_l[:, 0:32], pr, None, Op.is_equal)
-        n = ts(T.r1[:, :], pr, 1.0, None, Op.add)
-        vw(n)
-        ts(T.ct1[:, :], T.dg[:, :], -1.0, 1.0, Op.mult, Op.add)
-        ts(T.sc1[:, :], pr, 15.0, 1.0 - 2.0 ** -14, Op.is_equal, Op.mult)
-        n = ts(T.ct2[:, :], i32, T.r1[:, :], 16383.0, Op.is_equal, Op.mult)
-        vw(n)
-        done("v", V.tensor_tensor(T.ct[:, :], T.ct1[:, :], T.ct2[:, :], Op.add))
-        ts(T.scl[:, :], T.sc1[:, :], 2.0 ** -14, None, Op.add)
+        ts(T.mk[:, 0:32], T.p_l[:, 0:32], pr, None, Op.is_equal)
+        scan_consts()
         n_state = ts(T.gs[:, :], T.i_g[:, 0:128:16], pg, None, Op.is_equal)
-    ts(T.ex[0:16, :], T.i_r[0:16, :], T.col[0:16, 1:2], None, Op.is_equal)
-    n_fl = ts(T.ex8[0:16, :], T.i_r[0:16, :], T.col[0:16, 1:2], 8.0, Op.is_equal, Op.mult)
+    if is_rank:
+        ts(T.ex[0:16, :], T.i_r[0:16, :], T.col[0:16, 1:2], None, Op.is_equal)
+        n_fl = ts(T.ex8[0:16, :], T.i_r[0:16, :], T.col[0:16, 1:2], 8.0, Op.is_equal, Op.mult)
+    if comps:
+        n = ts(T.dfc[:, :], T.i_r[:, :], pp, None, Op.subtract)
+        vw(n)
+        for k in range(8):
+            n_rpc = ts(T.rpc[:, 128 * k:128 * k + 128], T.dfc[:, :], -16.0 * k, None, Op.is_equal)
 
-    if f != TOP:
-        arrived = bits(topo.mask(cores[TOP], cores[0]))
+    if maps:
         banks = {"next": 0}
         bank_free = [("a", 0)] * 4
         wready = {}
 
         def spread(m, parts, both):
-            PE.wait_ge(sem["m%d" % m], arrived)
+            if m >= N:
+                PE.wait_ge(sem.v, n_rpc)
+            PE.wait_ge(sem["m%d" % m], arrived if m < N else arrived * TEAMS[m - N][2])
             ready = {}
             per = 8 // parts
-            w = 64 * per
+            ww = 64 * per
+            mat = T.rp if m < N else T.rpc
             for h in range(parts):
                 b = banks["next"]
                 banks["next"] = (b + 1) % 4
@@ -203,67 +295,113 @@ def rank_program(g, core, T, topo):
                 n_pe = 0
                 for k in range(per):
                     kk = per * h + k
-                    n_pe = mm(0, ps[:, 64 * k:64 * k + 64], T.rp[:, 128 * kk:128 * kk + 128], land(T, m))
-                dst = win(T, m, w * h, w * h + w)
+                    n_pe = mm(0, ps[:, 64 * k:64 * k + 64], mat[:, 128 * kk:128 * kk + 128], land(T, m))
+                dst = win(T, m, ww * h, ww * h + ww)
                 if both and h % 2:
                     V.wait_ge(sem.pe, n_pe)
-                    bank_free[b] = ("v", done("v", V.tensor_copy(dst, ps[:, 0:w])))
+                    bank_free[b] = ("v", copy(dst, ps[:, 0:ww]))
                 else:
                     A.wait_ge(sem.pe, n_pe)
-                    bank_free[b] = ("a", done("a", A.activation(dst, ps[:, 0:w], Act.Copy)))
+                    bank_free[b] = ("a", done("a", A.activation(dst, ps[:, 0:ww], Act.Copy)))
                 ready[bank_free[b][0]] = bank_free[b][1]
             wready[m] = ready
 
-        maps = list(range(TOP, f, -1))
-        late = [m for m in maps if not topo.may_write(cores[m], core)]
-        first_late = late[0] if late else None
+        def straight_from(m):
+            return m < N and topo.may_write(cores[m], core)
 
-        def spread_late():
-            x = late.pop(0)
-            spread(x, 4 if x == first_late else 2, x == first_late)
-
+        n_rl = n_o = 0
+        if not is_rank:
+            m0 = TEAMS[team][0][0]
+            base = 64 * m0 + 2 * nc * part
+            mine = T.land[:, base:base + 2 * nc]
+            PE.wait_ge(sem.v, n_reord)
+            PE.wait_ge(sem["m%d" % m0], arrived)
+            n_o = mm(0, T.p_h[:, 0:2 * nc], T.reord[:, :], mine)
+            V.wait_ge(sem["m%d" % m0], arrived)
+            vw(n_state)
+            n_rl = done("v", V.tensor_tensor(T.rl[:, 0:w], mine.indirect(T.cof[:, 0:nc]), T.dgx[:, 0:w], Op.mult))
         PE.wait_ge(sem.v, n_rp)
-        for m in maps:
-            if m not in late:
-                spread(m, 2, False)
+        todo = list(maps)
+        for m in [x for x in todo[:EARLY] if straight_from(x)]:
+            todo.remove(m)
+            spread(m, 2, False)
+        if not is_rank:
+            n_pl = mm(n_rl, T.p_l[:, 0:w], T.bdx[:, :], T.rl[:, 0:w])
+            V.wait_ge(sem.pe, n_o)
+            copy(T.offs[:, 0:nc], T.p_h[:, 0:2 * nc:2])
+            V.wait_ge(sem.pe, n_pl)
+            n_state = ts(T.mk[:, 0:w], T.p_l[:, 0:w], pr, None, Op.is_equal)
+        fast = {"next": True}
+
+        def spread_next():
+            x = todo.pop(0)
+            quick = fast["next"] or x in comps[:1]
+            fast["next"] = False
+            spread(x, 4 if quick else 2, quick)
+
         nh = nl = 0
-        for m in maps:
+        for i in range(len(maps)):
+            m = maps[i]
             while m not in wready:
-                spread_late()
-            if m == first_late and late and late[0] == m - 1:
-                spread_late()
+                spread_next()
+            if i > 0 and todo and todo[0] == maps[min(i + 1, len(maps) - 1)] and todo[0] not in comps[:1]:
+                spread_next()
             for key in wready[m]:
                 V.wait_ge(sem[key], wready[m][key])
             vw(n_state)
-            o = T.offs[:, 0:2]
-            nh = done("v", V.tensor_tensor(T.xh[:, :], win(T, m, 0, 511).indirect(o), T.mk[:, :], Op.mult))
-            nl = done("v", V.tensor_tensor(T.xl[:, :], win(T, m, 1, 512).indirect(o), T.mk[:, :], Op.mult))
-            if m > f + 1:
-                h = mm(nh, T.p_h[:, 0:32], T.bd[:, :], T.xh[:, :])
-                l = mm(nl, T.p_l[:, 0:32], T.bd[:, :], T.xl[:, :])
+            o = T.offs[:, 0:nc]
+            nh = done("v", V.tensor_tensor(T.xh[:, 0:w], win(T, m, 0, 511).indirect(o), T.mk[:, 0:w], Op.mult))
+            nl = done("v", V.tensor_tensor(T.xl[:, 0:w], win(T, m, 1, 512).indirect(o), T.mk[:, 0:w], Op.mult))
+            if i + 1 < len(maps):
+                h = mm(nh, T.p_h[:, 0:w], T.bd[:, :], T.xh[:, 0:w])
+                l = mm(nl, T.p_l[:, 0:w], T.bd[:, :], T.xl[:, 0:w])
                 V.wait_ge(sem.pe, h)
-                n = done("v", V.tensor_tensor_scan(T.scn[:, :], T.ct[:, :], T.p_h[:, 0:32], 0.0, Op.mult, Op.add))
+                n = done("v", V.tensor_tensor_scan(T.scn[:, 0:w], T.ct[:, 0:w], T.p_h[:, 0:w], 0.0, Op.mult, Op.add))
                 V.wait_ge(sem.pe, l)
-                ts(T.mk[:, :], T.p_l[:, 0:32], pr, None, Op.is_equal)
+                ts(T.mk[:, 0:w], T.p_l[:, 0:w], pr, None, Op.is_equal)
                 vw(n)
-                n_state = ts(T.offs[:, :], T.scn[:, 15:32:16], T.scl[:, :], None, Op.mult)
-                if late:
-                    spread_late()
+                n_state = ts(T.offs[:, 0:nc], T.scn[:, 15:w:16], T.scl[:, :], None, Op.mult)
+
+        if not is_rank:
+            mm(nh, T.p_h[:, 0:w], T.bd[:, :], T.xh[:, 0:w])
+            l = mm(nl, T.p_h[:, w:2 * w], T.bd[:, :], T.xl[:, 0:w])
+            V.wait_ge(sem.pe, l)
+            n = done("v", V.tensor_tensor_scan(T.scn[:, 0:2 * w], T.ct[:, 0:2 * w], T.p_h[:, 0:2 * w], 0.0,
+                                               Op.mult, Op.add))
+            vw(n)
+            ts(T.emu[:, 0:2 * nc:2], T.scn[:, 15:w:16], T.scl[:, :], None, Op.mult)
+            n = ts(T.emu[:, 1:2 * nc:2], T.scn[:, w + 15:2 * w:16], T.scl[:, :], None, Op.mult)
+            vw(n)
+            g.wait_ge(sem.v, copy(T.em[:, 0:2 * nc], T.emu[:, 0:2 * nc]))
+            ranks = TEAMS[team][1]
+            a = 64 * (N + team) + 2 * nc * part
+            ids = []
+            for r in ranks:
+                rid, pid = topo.addr(cores[r], core)
+                ids.append(DstId(rid=rid, pnc=pid))
+            mask = topo.mask(core, cores[ranks[0]])
+            g.remote_dma_fused([RemoteDMATransfer(dst_ids=ids, dma_engine_mask=mask, remote_sem=sem["m%d" % (N + team)],
+                                                  srcs=[T.em[:, 0:2 * nc]],
+                                                  dsts=[T.land[:, a:a + 2 * nc] for r in ranks])], local_sem=sem.sa)
+            for key in ("v", "pe", "a", "gi"):
+                g.wait_ge(sem[key], cnt[key])
+            g.wait_ge(sem.sa, bits(mask))
+            return
         for c in range(2):
             mm(nh if c == 0 else 0, T.p_f[0:16, c:16:2], T.xh[:, 16 * c:16 * c + 16], T.gs[:, :])
         for c in range(2):
             n = mm(nl if c == 0 else 0, T.p_f[0:16, 16 + c:32:2], T.xl[:, 16 * c:16 * c + 16], T.gs[:, :])
         V.wait_ge(sem.pe, n)
-        n_fl = done("v", V.tensor_copy(T.fl[0:16, :], T.p_f[0:16, 0:32]))
+        n_fl = copy(T.fl[0:16, :], T.p_f[0:16, 0:32])
 
     mm(n_fl, T.p_g[:, 0:16], T.ex8[0:16, :], T.fl[0:16, 0:16], True, False)
     n = mm(0, T.p_g[:, 0:16], T.ex[0:16, :], T.fl[0:16, 16:32], False, True)
     V.wait_ge(sem.pe, n)
-    n_fo = done("v", V.tensor_copy(T.fo[:, :], T.p_g[:, 0:16]))
+    n_fo = copy(T.fo[:, :], T.p_g[:, 0:16])
 
     V.wait_ge(sem.dtab, 16)
     vw(n_fo)
-    n_ya = done("v", V.tensor_copy(T.ya[:, :], T.tb[:, :].indirect(T.fo[:, 0:8])))
+    n_ya = copy(T.ya[:, :], T.tb[:, :].indirect(T.fo[:, 0:8]))
     A.wait_ge(sem.dtab, 16)
     A.wait_ge(sem.v, n_fo)
     n_yb = done("a", A.activation(T.yb[:, :], T.tb[:, :].indirect(T.fo[:, 8:16]), Act.Copy))
@@ -272,7 +410,7 @@ def rank_program(g, core, T, topo):
     A.wait_ge(sem.a, n_yb)
     A.dma_start(T.y[:, 128:256], T.yb[:, :]).then_inc(sem.dyb, 16)
 
-    for key in ("v", "pe", "a"):
+    for key in ("v", "pe", "a", "gi"):
         g.wait_ge(sem[key], cnt[key])
     if n_sent:
         g.wait_ge(sem.sa, n_sent)

@@ -3,8 +3,10 @@ from concourse.mybir import AluOpType as Op, ActivationFunctionType as Act
 
 N = 12
 TOP = N - 1
-TEAMS = (((5, 4), (0, 1, 2, 3), 4), ((3, 2), (0, 1), 4))
-SLOTS = N + len(TEAMS)
+TEAMS = (((5, 4, 3), ((2, (0, 1, 3)), (3, (2,))), 4),
+         ((3, 2, 1), ((2, (1,)), (3, (0,))), 4))
+COMPS = [(_t, _maps[:_n], _ranks) for _t, (_maps, _outs, _h) in enumerate(TEAMS) for _n, _ranks in _outs]
+SLOTS = N + len(COMPS)
 EARLY = 4
 SCRATCH = {
     "land": ("sbuf", [128, 64 * SLOTS], "bfloat16"),
@@ -12,19 +14,19 @@ SCRATCH = {
     "tb": ("sbuf", [128, 4096], "bfloat16"),
 }
 for _name, _w, _t in (
-        ("raw", 32, "int32"), ("sp", 64, "int32"), ("pidx", 1, "int32"), ("pgr", 5, "int32"),
-        ("col", 5, "float32"), ("mi", 128, "int32"), ("mr", 128, "int32"), ("mg", 128, "int32"),
+        ("raw", 32, "int32"), ("sp", 64, "int32"), ("pidx", 1, "int32"), ("pgr", 4, "int32"),
+        ("col", 4, "float32"), ("mi", 128, "int32"), ("mr", 128, "int32"), ("mg", 128, "int32"),
         ("cof", 8, "uint16"), ("coi", 8, "int32"), ("df", 128, "bfloat16"), ("dfc", 128, "bfloat16"),
-        ("i_r", 128, "bfloat16"), ("i_g", 128, "bfloat16"),
+        ("i_r", 128, "bfloat16"), ("i_g", 128, "bfloat16"), ("i_q", 128, "bfloat16"),
         ("rp", 1024, "bfloat16"), ("rpc", 1024, "bfloat16"), ("reord", 128, "bfloat16"),
         ("bd", 128, "bfloat16"), ("bdx", 128, "bfloat16"), ("ex", 128, "bfloat16"), ("ex8", 128, "bfloat16"),
-        ("dg", 128, "bfloat16"), ("dgx", 128, "bfloat16"), ("ct1", 128, "float32"), ("ct2", 128, "float32"),
-        ("ct", 256, "float32"),
+        ("dg", 32, "bfloat16"), ("dgx", 128, "bfloat16"), ("ct1", 128, "float32"), ("ct2", 128, "float32"),
+        ("ct", 128, "float32"),
         ("r1", 1, "float32"), ("sc1", 1, "float32"), ("scl", 1, "float32"), ("gs", 8, "bfloat16"),
         ("wr", 16, "int32"), ("wsp", 32, "int32"), ("lof", 2, "float32"), ("rl", 128, "bfloat16"),
         ("offs", 8, "uint16"), ("mk", 128, "bfloat16"), ("xl", 128, "bfloat16"), ("xh", 128, "bfloat16"),
         ("scn", 256, "float32"), ("fl", 32, "bfloat16"), ("fo", 16, "uint16"),
-        ("emu", 16, "uint16"), ("em", 16, "bfloat16"),
+        ("emu", 64, "uint16"), ("em", 64, "bfloat16"),
         ("ya", 128, "bfloat16"), ("yb", 128, "bfloat16")):
     SCRATCH[_name] = ("sbuf", [128, _w], _t)
 for _name in ("p_l", "p_h", "p_f", "p_g", "p_r0", "p_r1", "p_r2", "p_r3"):
@@ -51,7 +53,8 @@ def place(topo, c):
 def team_cores(cores, topo):
     taken = set(place(topo, c) for c in cores)
     used, out = set(), []
-    for t, (maps, ranks, n) in enumerate(TEAMS):
+    for t, (maps, outs, n) in enumerate(TEAMS):
+        ranks = [r for n_maps, rs in outs for r in rs]
         fits = [c for c in range(256) if place(topo, c) not in taken and c not in used
                 and topo.die(c) == topo.die(cores[0]) and topo.same_plane(cores[maps[0]], c)
                 and all(topo.may_write(c, cores[r]) for r in ranks)]
@@ -69,10 +72,10 @@ def team_cores(cores, topo):
 
 def chain(f):
     out = list(range(TOP, f, -1))
-    for t, (maps, ranks, n) in enumerate(TEAMS):
+    for x, (t, maps, ranks) in enumerate(COMPS):
         if f in ranks:
             i = out.index(maps[0])
-            out[i:i + len(maps)] = [N + t]
+            out[i:i + len(maps)] = [N + x]
     return out
 
 
@@ -94,13 +97,15 @@ def receivers(f, cores, topo, teams):
     return straight, relay, groups
 
 
-def send(g, src, dsts, f, T, topo, mask):
+def send(g, src, dsts, m, T, topo, mask, what=None, where=None):
+    what = land(T, m) if what is None else what
+    where = land(T, m) if where is None else where
     ids = []
     for d in dsts:
         rid, pid = topo.addr(d, src)
         ids.append(DstId(rid=rid, pnc=pid))
-    g.remote_dma_fused([RemoteDMATransfer(dst_ids=ids, dma_engine_mask=mask, remote_sem=T.sem["m%d" % f],
-                                          srcs=[land(T, f)], dsts=[land(T, f) for d in dsts])],
+    g.remote_dma_fused([RemoteDMATransfer(dst_ids=ids, dma_engine_mask=mask, remote_sem=T.sem["m%d" % m],
+                                          srcs=[what], dsts=[where for d in dsts])],
                        local_sem=T.sem.sa)
     return bits(mask)
 
@@ -173,9 +178,13 @@ def rank_program(g, core, T, topo):
         g.sync.dma_start(T.tb[:, :], T.tab[:, :]).then_inc(sem.dtab, 16)
 
     done("gi", g.iota(T.pidx[:, :], [[0, 1]], 0, 1))
-    done("gi", g.iota(T.mi[:, :], [[1, 128]], 0, 0))
-    if not is_rank:
+    if is_rank:
+        done("gi", g.iota(T.mi[:, :], [[1, 128]], 0, 0))
+    else:
         done("gi", g.iota(T.coi[:, 0:nc], [[2, nc]], 1, 0))
+        for t, pattern, mul in ((T.i_r, [[0, 8], [1, 16]], 0), (T.i_g, [[1, 8], [0, 16]], 0),
+                                (T.df, [[0, 8], [8, 16]], -1), (T.i_q, [[1, 8], [8, 16]], -1)):
+            done("gi", g.iota(t[:, :], pattern, 0, mul, allow_small_or_imprecise_dtypes=True))
 
     n_sent = 0
     if is_rank and f > 0:
@@ -190,57 +199,60 @@ def rank_program(g, core, T, topo):
         for grp in straight:
             n_sent += send(g, core, grp, f, T, topo, topo.mask(core, grp[0]))
 
-    V.wait_ge(sem.gi, cnt["gi"])
+    V.wait_ge(sem.gi, 2)
     ts(T.pgr[:, 0:1], T.pidx[:, :], 4, None, Op.arith_shift_right)
     ts(T.pgr[:, 1:2], T.pidx[:, :], 15, None, Op.bitwise_and)
-    ts(T.mr[:, :], T.mi[:, :], 15, None, Op.bitwise_and)
-    ts(T.mg[:, :], T.mi[:, :], 4, None, Op.arith_shift_right)
-    npg = 3
-    if not is_rank:
-        npg = 5
-        ts(T.pgr[:, 3:4], T.pidx[:, :], 3, None, Op.arith_shift_right)
-        ts(T.pgr[:, 4:5], T.pidx[:, :], 7, None, Op.bitwise_and)
-    n = copy(T.pgr[:, 2:3], T.pidx[:, :])
-    vw(n)
-    copy(T.i_r[:, :], T.mr[:, :])
-    copy(T.i_g[:, :], T.mg[:, :])
+    if is_rank:
+        npg = 3
+        ts(T.mr[:, :], T.mi[:, :], 15, None, Op.bitwise_and)
+        ts(T.mg[:, :], T.mi[:, :], 4, None, Op.arith_shift_right)
+        n = copy(T.pgr[:, 2:3], T.pidx[:, :])
+        vw(n)
+        copy(T.i_r[:, :], T.mr[:, :])
+        copy(T.i_g[:, :], T.mg[:, :])
+    else:
+        npg = 4
+        ts(T.pgr[:, 2:3], T.pidx[:, :], 3, None, Op.arith_shift_right)
+        n = ts(T.pgr[:, 3:4], T.pidx[:, :], 7, None, Op.bitwise_and)
+        copy(T.cof[:, 0:nc], T.coi[:, 0:nc])
+        vw(n)
     n_col = copy(T.col[:, 0:npg], T.pgr[:, 0:npg])
     pg, pr, pp = T.col[:, 0:1], T.col[:, 1:2], T.col[:, 2:3]
     iw = T.i_r[:, 0:w]
     vw(n_col)
-    ts(T.dg[:, 0:w], iw, pr, None, Op.is_equal)
-    n_df = ts(T.df[:, :], T.i_r[:, :], 8.0, pp, Op.mult, Op.subtract)
-    ts(T.bd[:, :], T.i_g[:, :], pg, None, Op.is_equal)
+    n_df = 0
+    if is_rank:
+        ts(T.dg[:, 0:w], iw, pr, None, Op.is_equal)
+        n_df = ts(T.df[:, :], T.i_r[:, :], 8.0, pp, Op.mult, Op.subtract)
+        ts(T.bd[:, :], T.i_g[:, :], pg, None, Op.is_equal)
 
     def spread_consts():
-        vw(n_df)
+        if n_df:
+            vw(n_df)
         for k in range(8):
             n = ts(T.rp[:, 128 * k:128 * k + 128], T.df[:, :], -float(k), None, Op.is_equal)
         return n
 
     def scan_consts():
         n = ts(T.r1[:, :], pr, 1.0, None, Op.add)
+        ts(T.ct1[:, 0:w], iw, pr, None, Op.not_equal)
         vw(n)
-        ts(T.ct1[:, 0:w], T.dg[:, 0:w], -1.0, 1.0, Op.mult, Op.add)
         ts(T.sc1[:, :], pr, 15.0, 1.0 - 2.0 ** -14, Op.is_equal, Op.mult)
         n = ts(T.ct2[:, 0:w], iw, T.r1[:, :], 16383.0, Op.is_equal, Op.mult)
         vw(n)
         done("v", V.tensor_tensor(T.ct[:, 0:w], T.ct1[:, 0:w], T.ct2[:, 0:w], Op.add))
-        if not is_rank:
-            done("v", V.tensor_tensor(T.ct[:, w:2 * w], T.ct1[:, 0:w], T.ct2[:, 0:w], Op.add))
         return ts(T.scl[:, :], T.sc1[:, :], 2.0 ** -14, None, Op.add)
 
     n_rp = n_rpc = n_reord = n_state = n_fl = 0
     if not is_rank:
-        copy(T.cof[:, 0:nc], T.coi[:, 0:nc])
-        ts(T.dgx[:, 0:w], iw, T.col[:, 3:4], None, Op.is_equal)
-        ts(T.bdx[:, :], T.i_g[:, :], T.col[:, 4:5], None, Op.is_equal)
-        vw(n_df)
-        n = done("v", V.tensor_tensor(T.ct1[:, 0:128], T.df[:, :], T.i_g[:, :], Op.add))
-        vw(n)
-        n_reord = ts(T.reord[:, :], T.ct1[:, 0:128], 0.0, None, Op.is_equal)
-        n_rp = spread_consts()
+        V.wait_ge(sem.gi, 4)
+        ts(T.dgx[:, 0:w], iw, T.col[:, 2:3], None, Op.is_equal)
+        ts(T.bdx[:, :], T.i_g[:, :], T.col[:, 3:4], None, Op.is_equal)
+        ts(T.bd[:, :], T.i_g[:, :], pg, None, Op.is_equal)
         n_state = scan_consts()
+        V.wait_ge(sem.gi, 6)
+        n_reord = ts(T.reord[:, :], T.i_q[:, :], 0.0, None, Op.is_equal)
+        n_rp = spread_consts()
     elif f == TOP:
         V.wait_ge(sem.dst, 16)
         ts(T.wsp[0:16, 0:16], T.wr[0:16, :], 3, 510, Op.arith_shift_right, Op.bitwise_and)
@@ -280,7 +292,7 @@ def rank_program(g, core, T, topo):
         def spread(m, parts, both):
             if m >= N:
                 PE.wait_ge(sem.v, n_rpc)
-            PE.wait_ge(sem["m%d" % m], arrived if m < N else arrived * TEAMS[m - N][2])
+            PE.wait_ge(sem["m%d" % m], arrived if m < N else arrived * TEAMS[COMPS[m - N][0]][2])
             ready = {}
             per = 8 // parts
             ww = 64 * per
@@ -335,7 +347,7 @@ def rank_program(g, core, T, topo):
 
         def spread_next():
             x = todo.pop(0)
-            quick = fast["next"] or x in comps[:1]
+            quick = fast["next"]
             fast["next"] = False
             spread(x, 4 if quick else 2, quick)
 
@@ -344,7 +356,7 @@ def rank_program(g, core, T, topo):
             m = maps[i]
             while m not in wready:
                 spread_next()
-            if i > 0 and todo and todo[0] == maps[min(i + 1, len(maps) - 1)] and todo[0] not in comps[:1]:
+            if i > 0 and todo and todo[0] == maps[min(i + 1, len(maps) - 1)]:
                 spread_next()
             for key in wready[m]:
                 V.wait_ge(sem[key], wready[m][key])
@@ -352,40 +364,34 @@ def rank_program(g, core, T, topo):
             o = T.offs[:, 0:nc]
             nh = done("v", V.tensor_tensor(T.xh[:, 0:w], win(T, m, 0, 511).indirect(o), T.mk[:, 0:w], Op.mult))
             nl = done("v", V.tensor_tensor(T.xl[:, 0:w], win(T, m, 1, 512).indirect(o), T.mk[:, 0:w], Op.mult))
-            if i + 1 < len(maps):
+            out = [x for x in range(len(COMPS)) if not is_rank and COMPS[x][0] == team and len(COMPS[x][1]) == i + 2]
+            if i + 1 < len(maps) or out:
                 h = mm(nh, T.p_h[:, 0:w], T.bd[:, :], T.xh[:, 0:w])
                 l = mm(nl, T.p_l[:, 0:w], T.bd[:, :], T.xl[:, 0:w])
                 V.wait_ge(sem.pe, h)
                 n = done("v", V.tensor_tensor_scan(T.scn[:, 0:w], T.ct[:, 0:w], T.p_h[:, 0:w], 0.0, Op.mult, Op.add))
                 V.wait_ge(sem.pe, l)
+            if i + 1 < len(maps):
                 ts(T.mk[:, 0:w], T.p_l[:, 0:w], pr, None, Op.is_equal)
                 vw(n)
                 n_state = ts(T.offs[:, 0:nc], T.scn[:, 15:w:16], T.scl[:, :], None, Op.mult)
-
+            for x in out:
+                n2 = done("v", V.tensor_tensor_scan(T.scn[:, w:2 * w], T.ct[:, 0:w], T.p_l[:, 0:w], 0.0,
+                                                    Op.mult, Op.add))
+                e = 16 * x
+                vw(n)
+                ts(T.emu[:, e:e + 2 * nc:2], T.scn[:, 15:w:16], T.scl[:, :], None, Op.mult)
+                vw(n2)
+                n = ts(T.emu[:, e + 1:e + 2 * nc:2], T.scn[:, w + 15:2 * w:16], T.scl[:, :], None, Op.mult)
+                vw(n)
+                g.wait_ge(sem.v, copy(T.em[:, e:e + 2 * nc], T.emu[:, e:e + 2 * nc]))
+                a = 64 * (N + x) + 2 * nc * part
+                n_sent += send(g, core, [cores[r] for r in COMPS[x][2]], N + x, T, topo, off_mask,
+                               T.em[:, e:e + 2 * nc], T.land[:, a:a + 2 * nc])
         if not is_rank:
-            mm(nh, T.p_h[:, 0:w], T.bd[:, :], T.xh[:, 0:w])
-            l = mm(nl, T.p_h[:, w:2 * w], T.bd[:, :], T.xl[:, 0:w])
-            V.wait_ge(sem.pe, l)
-            n = done("v", V.tensor_tensor_scan(T.scn[:, 0:2 * w], T.ct[:, 0:2 * w], T.p_h[:, 0:2 * w], 0.0,
-                                               Op.mult, Op.add))
-            vw(n)
-            ts(T.emu[:, 0:2 * nc:2], T.scn[:, 15:w:16], T.scl[:, :], None, Op.mult)
-            n = ts(T.emu[:, 1:2 * nc:2], T.scn[:, w + 15:2 * w:16], T.scl[:, :], None, Op.mult)
-            vw(n)
-            g.wait_ge(sem.v, copy(T.em[:, 0:2 * nc], T.emu[:, 0:2 * nc]))
-            ranks = TEAMS[team][1]
-            a = 64 * (N + team) + 2 * nc * part
-            ids = []
-            for r in ranks:
-                rid, pid = topo.addr(cores[r], core)
-                ids.append(DstId(rid=rid, pnc=pid))
-            mask = topo.mask(core, cores[ranks[0]])
-            g.remote_dma_fused([RemoteDMATransfer(dst_ids=ids, dma_engine_mask=mask, remote_sem=sem["m%d" % (N + team)],
-                                                  srcs=[T.em[:, 0:2 * nc]],
-                                                  dsts=[T.land[:, a:a + 2 * nc] for r in ranks])], local_sem=sem.sa)
             for key in ("v", "pe", "a", "gi"):
                 g.wait_ge(sem[key], cnt[key])
-            g.wait_ge(sem.sa, bits(mask))
+            g.wait_ge(sem.sa, n_sent)
             return
         for c in range(2):
             mm(nh if c == 0 else 0, T.p_f[0:16, c:16:2], T.xh[:, 16 * c:16 * c + 16], T.gs[:, :])

@@ -3,11 +3,14 @@ from concourse.mybir import AluOpType as Op, ActivationFunctionType as Act
 
 N = 12
 TOP = N - 1
-TEAMS = (((5, 4, 3), ((2, (0, 1, 3)), (3, (2,))), 4),
+TEAMS = (((7, 6), ((2, (0, 1, 2, 3)),), 4),
+         ((5, 4, 3), ((2, (0, 1, 3)), (3, (2,))), 4),
          ((3, 2, 1), ((2, (1,)), (3, (0,))), 4))
 COMPS = [(_t, _maps[:_n], _ranks) for _t, (_maps, _outs, _h) in enumerate(TEAMS) for _n, _ranks in _outs]
 SLOTS = N + len(COMPS)
 EARLY = 4
+LIFT = 2.0
+FAR = 2.0 ** 30
 SCRATCH = {
     "land": ("sbuf", [128, 64 * SLOTS], "bfloat16"),
     "win": ("sbuf", [128, 512 * SLOTS], "bfloat16"),
@@ -15,18 +18,19 @@ SCRATCH = {
 }
 for _name, _w, _t in (
         ("raw", 32, "int32"), ("sp", 64, "int32"), ("pidx", 1, "int32"), ("pgr", 4, "int32"),
-        ("col", 4, "float32"), ("mi", 128, "int32"), ("mr", 128, "int32"), ("mg", 128, "int32"),
-        ("cof", 8, "uint16"), ("coi", 8, "int32"), ("df", 128, "bfloat16"), ("dfc", 128, "bfloat16"),
+        ("col", 4, "float32"),
+        ("cof", 8, "uint16"), ("coi", 8, "int32"), ("df", 128, "bfloat16"), ("ones", 256, "bfloat16"),
         ("i_r", 128, "bfloat16"), ("i_g", 128, "bfloat16"), ("i_q", 128, "bfloat16"),
         ("rp", 1024, "bfloat16"), ("rpc", 1024, "bfloat16"), ("reord", 128, "bfloat16"),
         ("bd", 128, "bfloat16"), ("bdx", 128, "bfloat16"), ("ex", 128, "bfloat16"), ("ex8", 128, "bfloat16"),
         ("dg", 32, "bfloat16"), ("dgx", 128, "bfloat16"), ("ct1", 128, "float32"), ("ct2", 128, "float32"),
-        ("ct", 128, "float32"),
-        ("r1", 1, "float32"), ("sc1", 1, "float32"), ("scl", 1, "float32"), ("gs", 8, "bfloat16"),
+        ("ct", 128, "float32"), ("prl", 1, "float32"),
+        ("r1", 1, "float32"), ("sc1", 1, "float32"), ("scl", 1, "float32"), ("gs", 16, "bfloat16"),
+        ("sel", 16, "bfloat16"),
         ("wr", 16, "int32"), ("wsp", 32, "int32"), ("lof", 2, "float32"), ("rl", 128, "bfloat16"),
-        ("offs", 8, "uint16"), ("mk", 128, "bfloat16"), ("xl", 128, "bfloat16"), ("xh", 128, "bfloat16"),
+        ("offs", 8, "uint16"), ("mk", 128, "bfloat16"), ("xx", 256, "bfloat16"),
         ("scn", 256, "float32"), ("fl", 32, "bfloat16"), ("fo", 16, "uint16"),
-        ("emu", 64, "uint16"), ("em", 64, "bfloat16"),
+        ("em", 16 * len(COMPS), "bfloat16"),
         ("ya", 128, "bfloat16"), ("yb", 128, "bfloat16")):
     SCRATCH[_name] = ("sbuf", [128, _w], _t)
 for _name in ("p_l", "p_h", "p_f", "p_g", "p_r0", "p_r1", "p_r2", "p_r3"):
@@ -50,23 +54,31 @@ def place(topo, c):
     return topo.host(c), topo.chip(c)
 
 
+def relay_of(src, cores, topo):
+    return [c for c in range(256) if c != src and place(topo, c) == place(topo, src)
+            and topo.die(c) == topo.die(src) and all(topo.may_write(c, d) for d in cores)][0]
+
+
 def team_cores(cores, topo):
-    taken = set(place(topo, c) for c in cores)
-    used, out = set(), []
+    used = set(place(topo, c) for c in cores)
+    posts = [relay_of(src, cores, topo) for src in cores[::-1]]
+    out = []
     for t, (maps, outs, n) in enumerate(TEAMS):
         ranks = [r for n_maps, rs in outs for r in rs]
-        fits = [c for c in range(256) if place(topo, c) not in taken and c not in used
+        if t == 0:
+            out.append([c for c in posts if topo.may_write(cores[maps[0]], c)][:n])
+            continue
+        fits = [c for c in range(256) if place(topo, c) not in used
                 and topo.die(c) == topo.die(cores[0]) and topo.same_plane(cores[maps[0]], c)
                 and all(topo.may_write(c, cores[r]) for r in ranks)]
-        team, seen = [], set()
+        team = []
         for c in (fits if t % 2 == 0 else fits[::-1]):
-            if place(topo, c) not in seen and len(team) < n:
+            if place(topo, c) not in used and len(team) < n:
                 team.append(c)
-                seen.add(place(topo, c))
-        if len(team) < n:
-            raise ValueError("no team")
-        used |= set(team)
+                used.add(place(topo, c))
         out.append(team)
+    if any(len(team) < n for team, (maps, outs, n) in zip(out, TEAMS)):
+        raise ValueError("no team")
     return out
 
 
@@ -91,8 +103,9 @@ def receivers(f, cores, topo, teams):
     far = [d for d in ranks if not ok(src, d)] + [d for team in helpers for d in team if not ok(src, d)]
     relay, groups = None, []
     if far:
-        relay = [c for c in range(256) if c != src and place(topo, c) == place(topo, src)
-                 and topo.die(c) == topo.die(src) and all(ok(c, d) for d in far)][0]
+        relay = relay_of(src, cores, topo)
+        if (TOP - f) % 2 == 0:
+            far[:2] = far[1::-1]
         groups = [[d] for d in far[:2]] + [far[i:i + 2] for i in range(2, len(far), 2)]
     return straight, relay, groups
 
@@ -110,37 +123,38 @@ def send(g, src, dsts, m, T, topo, mask, what=None, where=None):
     return bits(mask)
 
 
-def run_relay(g, core, f, groups, T, topo):
-    off = topo.mask(core, groups[0][0])
-    g.wait_ge(T.sem["m%d" % f], bits(off))
+def run_relay(g, core, cores, teams, T, topo, off):
     n = 0
-    for grp in groups:
-        n += send(g, core, grp, f, T, topo, off)
-    g.wait_ge(T.sem.sa, n)
+    for r in range(1, N):
+        straight, relay, groups = receivers(r, cores, topo, teams)
+        if relay == core:
+            g.wait_ge(T.sem["m%d" % r], bits(off))
+            for grp in groups:
+                n += send(g, core, grp, r, T, topo, off)
+    return n
 
 
 def rank_program(g, core, T, topo):
     cores = list(T.cores)
     f = T.rank_of(core)
     teams = team_cores(cores, topo)
+    off_mask = topo.mask(cores[TOP], cores[0])
+    arrived = bits(off_mask)
     is_rank = f is not None
     team = part = None
+    sem = T.sem
     if not is_rank:
         for t in range(len(TEAMS)):
             if core in teams[t]:
                 team, part = t, teams[t].index(core)
         if team is None:
-            for r in range(1, N):
-                straight, relay, groups = receivers(r, cores, topo, teams)
-                if relay == core:
-                    run_relay(g, core, r, groups, T, topo)
+            n = run_relay(g, core, cores, teams, T, topo, off_mask)
+            if n:
+                g.wait_ge(sem.sa, n)
             return
 
-    sem = T.sem
     cnt = {"v": 0, "pe": 0, "a": 0, "gi": 0}
     V, PE, A = g.vector, g.tensor, g.scalar
-    off_mask = topo.mask(cores[TOP], cores[0])
-    arrived = bits(off_mask)
 
     def done(key, ins):
         ins.then_inc(sem[key], 1)
@@ -163,8 +177,12 @@ def rank_program(g, core, T, topo):
 
     maps = chain(f) if is_rank else list(TEAMS[team][0][1:])
     comps = [m for m in maps if m >= N]
+    late = comps[:1] + [m for m in comps[1:] if len(COMPS[m - N][1]) > 2]
     nc = 2 if is_rank else 32 // TEAMS[team][2]
     w = 16 * nc
+
+    def straight_from(m):
+        return m < N and topo.may_write(cores[m], core)
 
     if is_rank:
         if f > 0:
@@ -178,15 +196,13 @@ def rank_program(g, core, T, topo):
         g.sync.dma_start(T.tb[:, :], T.tab[:, :]).then_inc(sem.dtab, 16)
 
     done("gi", g.iota(T.pidx[:, :], [[0, 1]], 0, 1))
-    if is_rank:
-        done("gi", g.iota(T.mi[:, :], [[1, 128]], 0, 0))
-    else:
+    if not is_rank:
         done("gi", g.iota(T.coi[:, 0:nc], [[2, nc]], 1, 0))
-        for t, pattern, mul in ((T.i_r, [[0, 8], [1, 16]], 0), (T.i_g, [[1, 8], [0, 16]], 0),
-                                (T.df, [[0, 8], [8, 16]], -1), (T.i_q, [[1, 8], [8, 16]], -1)):
-            done("gi", g.iota(t[:, :], pattern, 0, mul, allow_small_or_imprecise_dtypes=True))
+    for t, pattern, mul in ((T.i_r, [[0, 8], [1, 16]], 0), (T.i_g, [[1, 8], [0, 16]], 0)) + (
+            () if is_rank else ((T.df, [[0, 8], [8, 16]], -1), (T.i_q, [[1, 8], [8, 16]], -1))):
+        done("gi", g.iota(t[:, :], pattern, 0, mul, allow_small_or_imprecise_dtypes=True))
 
-    n_sent = 0
+    n_sent = 0 if is_rank else run_relay(g, core, cores, teams, T, topo, off_mask)
     if is_rank and f > 0:
         straight, relay, groups = receivers(f, cores, topo, teams)
         V.wait_ge(sem.dbp, 16)
@@ -194,29 +210,30 @@ def rank_program(g, core, T, topo):
         n = ts(T.sp[:, 1:64:2], T.raw[:, :], 15, None, Op.bitwise_and)
         vw(n)
         g.wait_ge(sem.v, copy(land(T, f), T.sp[:, :]))
-        if groups:
-            n_sent += send(g, core, [relay], f, T, topo, off_mask)
-        for grp in straight:
-            n_sent += send(g, core, grp, f, T, topo, topo.mask(core, grp[0]))
+        calls = [[relay]] if groups and all(relay not in grp for grp in straight) else []
+        if groups and straight and straight[0][0] not in cores and all(d in cores for grp in groups for d in grp):
+            calls = [straight.pop(0)] + calls
+        for grp in calls + straight:
+            n_sent += send(g, core, grp, f, T, topo, off_mask)
 
-    V.wait_ge(sem.gi, 2)
+    V.wait_ge(sem.gi, 3 if is_rank else 2)
     ts(T.pgr[:, 0:1], T.pidx[:, :], 4, None, Op.arith_shift_right)
     ts(T.pgr[:, 1:2], T.pidx[:, :], 15, None, Op.bitwise_and)
+    n_rpc = 0
     if is_rank:
-        npg = 3
-        ts(T.mr[:, :], T.mi[:, :], 15, None, Op.bitwise_and)
-        ts(T.mg[:, :], T.mi[:, :], 4, None, Op.arith_shift_right)
+        if comps:
+            g.wait_ge(sem.v, done("v", V.memset(T.ones[:, :], 1.0)))
+            for k in range(0, 8, 2):
+                n_rpc = done("gi", g.affine_select(T.rpc[:, 128 * k:128 * k + 256], T.ones[:, :],
+                                                   [[-16, 2], [0, 8], [-1, 16]], Op.is_equal, 0.0, -16 * k, 1))
+        ts(T.pgr[:, 3:4], T.pidx[:, :], 4, 1, Op.arith_shift_right, Op.bitwise_and)
         n = copy(T.pgr[:, 2:3], T.pidx[:, :])
-        vw(n)
-        copy(T.i_r[:, :], T.mr[:, :])
-        copy(T.i_g[:, :], T.mg[:, :])
     else:
-        npg = 4
+        copy(T.cof[:, 0:nc], T.coi[:, 0:nc])
         ts(T.pgr[:, 2:3], T.pidx[:, :], 3, None, Op.arith_shift_right)
         n = ts(T.pgr[:, 3:4], T.pidx[:, :], 7, None, Op.bitwise_and)
-        copy(T.cof[:, 0:nc], T.coi[:, 0:nc])
-        vw(n)
-    n_col = copy(T.col[:, 0:npg], T.pgr[:, 0:npg])
+    vw(n)
+    n_col = copy(T.col[:, :], T.pgr[:, :])
     pg, pr, pp = T.col[:, 0:1], T.col[:, 1:2], T.col[:, 2:3]
     iw = T.i_r[:, 0:w]
     vw(n_col)
@@ -235,15 +252,24 @@ def rank_program(g, core, T, topo):
 
     def scan_consts():
         n = ts(T.r1[:, :], pr, 1.0, None, Op.add)
+        ts(T.prl[:, :], pr, LIFT, None, Op.add)
         ts(T.ct1[:, 0:w], iw, pr, None, Op.not_equal)
         vw(n)
-        ts(T.sc1[:, :], pr, 15.0, 1.0 - 2.0 ** -14, Op.is_equal, Op.mult)
-        n = ts(T.ct2[:, 0:w], iw, T.r1[:, :], 16383.0, Op.is_equal, Op.mult)
+        ts(T.sc1[:, :], pr, 15.0, 1.0 - 1.0 / FAR, Op.is_equal, Op.mult)
+        n = ts(T.ct2[:, 0:w], iw, T.r1[:, :], FAR, Op.is_equal, Op.mult)
         vw(n)
         done("v", V.tensor_tensor(T.ct[:, 0:w], T.ct1[:, 0:w], T.ct2[:, 0:w], Op.add))
-        return ts(T.scl[:, :], T.sc1[:, :], 2.0 ** -14, None, Op.add)
+        return ts(T.scl[:, :], T.sc1[:, :], 1.0 / FAR, None, Op.add)
 
-    n_rp = n_rpc = n_reord = n_state = n_fl = 0
+    def end_consts():
+        if f == TOP:
+            ts(T.ex[0:16, :], T.i_r[0:16, :], T.col[0:16, 1:2], None, Op.is_equal)
+            return ts(T.ex8[0:16, :], T.i_r[0:16, :], T.col[0:16, 1:2], 8.0, Op.is_equal, Op.mult)
+        ts(T.sel[:, :], T.i_r[:, 0:128:8], 0.125, T.col[:, 3:4], Op.mult, Op.is_equal)
+        ts(T.ex[0:w, :], T.i_r[0:w, :], T.col[0:w, 1:2], 8.0, Op.is_equal, Op.mult)
+        return ts(T.ex[w:2 * w, :], T.i_r[w:2 * w, :], T.col[w:2 * w, 1:2], None, Op.is_equal)
+
+    n_rp = n_reord = n_state = n_fl = 0
     if not is_rank:
         V.wait_ge(sem.gi, 4)
         ts(T.dgx[:, 0:w], iw, T.col[:, 2:3], None, Op.is_equal)
@@ -274,15 +300,10 @@ def rank_program(g, core, T, topo):
         V.wait_ge(sem.pe, n_rl)
         ts(T.mk[:, 0:32], T.p_l[:, 0:32], pr, None, Op.is_equal)
         scan_consts()
-        n_state = ts(T.gs[:, :], T.i_g[:, 0:128:16], pg, None, Op.is_equal)
-    if is_rank:
-        ts(T.ex[0:16, :], T.i_r[0:16, :], T.col[0:16, 1:2], None, Op.is_equal)
-        n_fl = ts(T.ex8[0:16, :], T.i_r[0:16, :], T.col[0:16, 1:2], 8.0, Op.is_equal, Op.mult)
-    if comps:
-        n = ts(T.dfc[:, :], T.i_r[:, :], pp, None, Op.subtract)
-        vw(n)
-        for k in range(8):
-            n_rpc = ts(T.rpc[:, 128 * k:128 * k + 128], T.dfc[:, :], -16.0 * k, None, Op.is_equal)
+        n_state = ts(T.gs[:, :], T.i_g[:, 0:128:8], pg, None, Op.is_equal)
+    soon = bool(maps) and straight_from(maps[0])
+    if is_rank and not soon:
+        n_fl = end_consts()
 
     if maps:
         banks = {"next": 0}
@@ -291,7 +312,7 @@ def rank_program(g, core, T, topo):
 
         def spread(m, parts, both):
             if m >= N:
-                PE.wait_ge(sem.v, n_rpc)
+                PE.wait_ge(sem.gi, n_rpc)
             PE.wait_ge(sem["m%d" % m], arrived if m < N else arrived * TEAMS[COMPS[m - N][0]][2])
             ready = {}
             per = 8 // parts
@@ -318,9 +339,6 @@ def rank_program(g, core, T, topo):
                 ready[bank_free[b][0]] = bank_free[b][1]
             wready[m] = ready
 
-        def straight_from(m):
-            return m < N and topo.may_write(cores[m], core)
-
         n_rl = n_o = 0
         if not is_rank:
             m0 = TEAMS[team][0][0]
@@ -332,22 +350,23 @@ def rank_program(g, core, T, topo):
             V.wait_ge(sem["m%d" % m0], arrived)
             vw(n_state)
             n_rl = done("v", V.tensor_tensor(T.rl[:, 0:w], mine.indirect(T.cof[:, 0:nc]), T.dgx[:, 0:w], Op.mult))
+            V.wait_ge(sem.pe, n_o)
+            copy(T.offs[:, 0:nc], T.p_h[:, 0:2 * nc:2])
         PE.wait_ge(sem.v, n_rp)
         todo = list(maps)
         for m in [x for x in todo[:EARLY] if straight_from(x)]:
             todo.remove(m)
-            spread(m, 2, False)
-        if not is_rank:
-            n_pl = mm(n_rl, T.p_l[:, 0:w], T.bdx[:, :], T.rl[:, 0:w])
-            V.wait_ge(sem.pe, n_o)
-            copy(T.offs[:, 0:nc], T.p_h[:, 0:2 * nc:2])
-            V.wait_ge(sem.pe, n_pl)
-            n_state = ts(T.mk[:, 0:w], T.p_l[:, 0:w], pr, None, Op.is_equal)
+            first = m == maps[0]
+            spread(m, 4 if first else 2, first)
+            if not is_rank and first:
+                n_pl = mm(n_rl, T.p_l[:, 0:w], T.bdx[:, :], T.rl[:, 0:w])
+                V.wait_ge(sem.pe, n_pl)
+                n_state = ts(T.mk[:, 0:w], T.p_l[:, 0:w], pr, None, Op.is_equal)
         fast = {"next": True}
 
-        def spread_next():
+        def spread_next(idle):
             x = todo.pop(0)
-            quick = fast["next"]
+            quick = fast["next"] or idle
             fast["next"] = False
             spread(x, 4 if quick else 2, quick)
 
@@ -355,55 +374,60 @@ def rank_program(g, core, T, topo):
         for i in range(len(maps)):
             m = maps[i]
             while m not in wready:
-                spread_next()
-            if i > 0 and todo and todo[0] == maps[min(i + 1, len(maps) - 1)]:
-                spread_next()
+                spread_next(True)
+            if i > 0 and todo and todo[0] == maps[min(i + 1, len(maps) - 1)] and todo[0] not in late:
+                spread_next(False)
             for key in wready[m]:
                 V.wait_ge(sem[key], wready[m][key])
             vw(n_state)
             o = T.offs[:, 0:nc]
-            nh = done("v", V.tensor_tensor(T.xh[:, 0:w], win(T, m, 0, 511).indirect(o), T.mk[:, 0:w], Op.mult))
-            nl = done("v", V.tensor_tensor(T.xl[:, 0:w], win(T, m, 1, 512).indirect(o), T.mk[:, 0:w], Op.mult))
+            nh = done("v", V.tensor_tensor(T.xx[:, 0:w], win(T, m, 0, 511).indirect(o), T.mk[:, 0:w], Op.mult))
+            nl = done("v", V.tensor_tensor(T.xx[:, w:2 * w], win(T, m, 1, 512).indirect(o), T.mk[:, 0:w], Op.mult))
             out = [x for x in range(len(COMPS)) if not is_rank and COMPS[x][0] == team and len(COMPS[x][1]) == i + 2]
             if i + 1 < len(maps) or out:
-                h = mm(nh, T.p_h[:, 0:w], T.bd[:, :], T.xh[:, 0:w])
-                l = mm(nl, T.p_l[:, 0:w], T.bd[:, :], T.xl[:, 0:w])
+                h = mm(nh, T.p_h[:, 0:w], T.bd[:, :], T.xx[:, 0:w])
+                l = mm(nl, T.p_l[:, 0:w], T.bd[:, :], T.xx[:, w:2 * w])
                 V.wait_ge(sem.pe, h)
                 n = done("v", V.tensor_tensor_scan(T.scn[:, 0:w], T.ct[:, 0:w], T.p_h[:, 0:w], 0.0, Op.mult, Op.add))
                 V.wait_ge(sem.pe, l)
             if i + 1 < len(maps):
-                ts(T.mk[:, 0:w], T.p_l[:, 0:w], pr, None, Op.is_equal)
+                ts(T.mk[:, 0:w], T.p_l[:, 0:w], T.prl[:, :] if m >= N else pr, None, Op.is_equal)
                 vw(n)
                 n_state = ts(T.offs[:, 0:nc], T.scn[:, 15:w:16], T.scl[:, :], None, Op.mult)
+            if i == 0 and is_rank and soon:
+                end_consts()
             for x in out:
+                e = 16 * x
+                A.wait_ge(sem.v, n)
+                n_eh = done("a", A.activation(T.em[:, e:e + 2 * nc:2], T.scn[:, 15:w:16], Act.Copy,
+                                              scale=T.scl[:, :]))
                 n2 = done("v", V.tensor_tensor_scan(T.scn[:, w:2 * w], T.ct[:, 0:w], T.p_l[:, 0:w], 0.0,
                                                     Op.mult, Op.add))
-                e = 16 * x
-                vw(n)
-                ts(T.emu[:, e:e + 2 * nc:2], T.scn[:, 15:w:16], T.scl[:, :], None, Op.mult)
                 vw(n2)
-                n = ts(T.emu[:, e + 1:e + 2 * nc:2], T.scn[:, w + 15:2 * w:16], T.scl[:, :], None, Op.mult)
-                vw(n)
-                g.wait_ge(sem.v, copy(T.em[:, e:e + 2 * nc], T.emu[:, e:e + 2 * nc]))
+                n = ts(T.em[:, e + 1:e + 2 * nc:2], T.scn[:, w + 15:2 * w:16], T.scl[:, :], LIFT, Op.mult, Op.add)
+                g.wait_ge(sem.a, n_eh)
+                g.wait_ge(sem.v, n)
                 a = 64 * (N + x) + 2 * nc * part
-                n_sent += send(g, core, [cores[r] for r in COMPS[x][2]], N + x, T, topo, off_mask,
-                               T.em[:, e:e + 2 * nc], T.land[:, a:a + 2 * nc])
+                ranks = [cores[r] for r in COMPS[x][2]]
+                for k in range(0, len(ranks), 2):
+                    n_sent += send(g, core, ranks[k:k + 2], N + x, T, topo, off_mask,
+                                   T.em[:, e:e + 2 * nc], T.land[:, a:a + 2 * nc])
         if not is_rank:
             for key in ("v", "pe", "a", "gi"):
                 g.wait_ge(sem[key], cnt[key])
             g.wait_ge(sem.sa, n_sent)
             return
-        for c in range(2):
-            mm(nh if c == 0 else 0, T.p_f[0:16, c:16:2], T.xh[:, 16 * c:16 * c + 16], T.gs[:, :])
-        for c in range(2):
-            n = mm(nl if c == 0 else 0, T.p_f[0:16, 16 + c:32:2], T.xl[:, 16 * c:16 * c + 16], T.gs[:, :])
+        n = mm(nl, T.p_f[0:2 * w, 0:16], T.xx[:, 0:2 * w], T.gs[:, :])
         V.wait_ge(sem.pe, n)
-        n_fl = copy(T.fl[0:16, :], T.p_f[0:16, 0:32])
+        n_fl = done("v", V.tensor_tensor(T.fl[0:2 * w, 0:16], T.p_f[0:2 * w, 0:16], T.sel[0:2 * w, :], Op.mult))
 
-    mm(n_fl, T.p_g[:, 0:16], T.ex8[0:16, :], T.fl[0:16, 0:16], True, False)
-    n = mm(0, T.p_g[:, 0:16], T.ex[0:16, :], T.fl[0:16, 16:32], False, True)
+    if maps:
+        n = mm(n_fl, T.p_g[:, 0:16], T.ex[0:2 * w, :], T.fl[0:2 * w, 0:16])
+    else:
+        mm(n_fl, T.p_g[:, 0:16], T.ex8[0:16, :], T.fl[0:16, 0:16], True, False)
+        n = mm(0, T.p_g[:, 0:16], T.ex[0:16, :], T.fl[0:16, 16:32], False, True)
     V.wait_ge(sem.pe, n)
-    n_fo = copy(T.fo[:, :], T.p_g[:, 0:16])
+    n_fo = ts(T.fo[:, :], T.p_g[:, 0:16], -LIFT if maps and maps[-1] >= N else 0.0, None, Op.add)
 
     V.wait_ge(sem.dtab, 16)
     vw(n_fo)

from concourse.bass import DstId, RemoteDMATransfer
from concourse.mybir import AluOpType as Op, ActivationFunctionType as Act

N = 12
TOP = N - 1
TEAMS = (((7, 6), ((2, (0, 1, 2, 3)),), 4),
         ((5, 4, 3), ((2, (0, 1, 3)), (3, (2,))), 4),
         ((3, 2, 1), ((2, (1,)), (3, (0,))), 4))
COMPS = [(_t, _maps[:_n], _ranks) for _t, (_maps, _outs, _h) in enumerate(TEAMS) for _n, _ranks in _outs]
SLOTS = N + len(COMPS)
EARLY = 4
LIFT = 2.0
FAR = 2.0 ** 30
SCRATCH = {
    "land": ("sbuf", [128, 64 * SLOTS], "bfloat16"),
    "win": ("sbuf", [128, 512 * SLOTS], "bfloat16"),
    "tb": ("sbuf", [128, 4096], "bfloat16"),
}
for _name, _w, _t in (
        ("raw", 32, "int32"), ("sp", 64, "int32"), ("pidx", 1, "int32"), ("pgr", 4, "int32"),
        ("col", 4, "float32"),
        ("cof", 8, "uint16"), ("coi", 8, "int32"), ("df", 128, "bfloat16"), ("ones", 256, "bfloat16"),
        ("i_r", 128, "bfloat16"), ("i_g", 128, "bfloat16"), ("i_q", 128, "bfloat16"),
        ("rp", 1024, "bfloat16"), ("rpc", 1024, "bfloat16"), ("reord", 128, "bfloat16"),
        ("bd", 128, "bfloat16"), ("bdx", 128, "bfloat16"), ("ex", 128, "bfloat16"), ("ex8", 128, "bfloat16"),
        ("dg", 32, "bfloat16"), ("dgx", 128, "bfloat16"), ("ct1", 128, "float32"), ("ct2", 128, "float32"),
        ("ct", 128, "float32"), ("prl", 1, "float32"),
        ("r1", 1, "float32"), ("sc1", 1, "float32"), ("scl", 1, "float32"), ("gs", 16, "bfloat16"),
        ("sel", 16, "bfloat16"),
        ("wr", 16, "int32"), ("wsp", 32, "int32"), ("lof", 2, "float32"), ("rl", 128, "bfloat16"),
        ("offs", 8, "uint16"), ("mk", 128, "bfloat16"), ("xx", 256, "bfloat16"),
        ("scn", 256, "float32"), ("fl", 32, "bfloat16"), ("fo", 16, "uint16"),
        ("em", 16 * len(COMPS), "bfloat16"),
        ("ya", 128, "bfloat16"), ("yb", 128, "bfloat16")):
    SCRATCH[_name] = ("sbuf", [128, _w], _t)
for _name in ("p_l", "p_h", "p_f", "p_g", "p_r0", "p_r1", "p_r2", "p_r3"):
    SCRATCH[_name] = ("psum", [128, 512], "float32")
SEMAPHORES = ["v", "pe", "a", "gi", "dbp", "dst", "dtab", "dya", "dyb", "sa"] + ["m%d" % _m for _m in range(1, SLOTS)]


def land(T, m):
    return T.land[:, 64 * m:64 * m + 64]


def win(T, m, a, b):
    return T.win[:, 512 * m + a:512 * m + b]


def bits(mask):
    return bin(mask).count("1")


def place(topo, c):
    return topo.host(c), topo.chip(c)


def relay_of(src, cores, topo):
    return [c for c in range(256) if c != src and place(topo, c) == place(topo, src)
            and topo.die(c) == topo.die(src) and all(topo.may_write(c, d) for d in cores)][0]


def team_cores(cores, topo):
    used = set(place(topo, c) for c in cores)
    posts = [relay_of(src, cores, topo) for src in cores[::-1]]
    out = []
    for t, (maps, outs, n) in enumerate(TEAMS):
        ranks = [r for n_maps, rs in outs for r in rs]
        if t == 0:
            out.append([c for c in posts if topo.may_write(cores[maps[0]], c)][:n])
            continue
        fits = [c for c in range(256) if place(topo, c) not in used
                and topo.die(c) == topo.die(cores[0]) and topo.same_plane(cores[maps[0]], c)
                and all(topo.may_write(c, cores[r]) for r in ranks)]
        team = []
        for c in (fits if t % 2 == 0 else fits[::-1]):
            if place(topo, c) not in used and len(team) < n:
                team.append(c)
                used.add(place(topo, c))
        out.append(team)
    if any(len(team) < n for team, (maps, outs, n) in zip(out, TEAMS)):
        raise ValueError("no team")
    return out


def chain(f):
    out = list(range(TOP, f, -1))
    for x, (t, maps, ranks) in enumerate(COMPS):
        if f in ranks:
            i = out.index(maps[0])
            out[i:i + len(maps)] = [N + x]
    return out


def receivers(f, cores, topo, teams):
    src = cores[f]
    ok = topo.may_write
    ranks = [cores[d] for d in range(f) if f in chain(d)]
    helpers = [teams[t] for t in range(len(TEAMS)) if f in TEAMS[t][0]]
    near_ranks = [d for d in ranks if ok(src, d)]
    straight = [[d for d in team if ok(src, d)] for team in helpers]
    straight += [near_ranks[i:i + 2] for i in range(0, len(near_ranks), 2)]
    straight = [grp for grp in straight if grp]
    far = [d for d in ranks if not ok(src, d)] + [d for team in helpers for d in team if not ok(src, d)]
    relay, groups = None, []
    if far:
        relay = relay_of(src, cores, topo)
        if (TOP - f) % 2 == 0:
            far[:2] = far[1::-1]
        groups = [[d] for d in far[:2]] + [far[i:i + 2] for i in range(2, len(far), 2)]
    return straight, relay, groups


def send(g, src, dsts, m, T, topo, mask, what=None, where=None):
    what = land(T, m) if what is None else what
    where = land(T, m) if where is None else where
    ids = []
    for d in dsts:
        rid, pid = topo.addr(d, src)
        ids.append(DstId(rid=rid, pnc=pid))
    g.remote_dma_fused([RemoteDMATransfer(dst_ids=ids, dma_engine_mask=mask, remote_sem=T.sem["m%d" % m],
                                          srcs=[what], dsts=[where for d in dsts])],
                       local_sem=T.sem.sa)
    return bits(mask)


def run_relay(g, core, cores, teams, T, topo, off):
    n = 0
    for r in range(1, N):
        straight, relay, groups = receivers(r, cores, topo, teams)
        if relay == core:
            g.wait_ge(T.sem["m%d" % r], bits(off))
            for grp in groups:
                n += send(g, core, grp, r, T, topo, off)
    return n


def rank_program(g, core, T, topo):
    cores = list(T.cores)
    f = T.rank_of(core)
    teams = team_cores(cores, topo)
    off_mask = topo.mask(cores[TOP], cores[0])
    arrived = bits(off_mask)
    is_rank = f is not None
    team = part = None
    sem = T.sem
    if not is_rank:
        for t in range(len(TEAMS)):
            if core in teams[t]:
                team, part = t, teams[t].index(core)
        if team is None:
            n = run_relay(g, core, cores, teams, T, topo, off_mask)
            if n:
                g.wait_ge(sem.sa, n)
            return

    cnt = {"v": 0, "pe": 0, "a": 0, "gi": 0}
    V, PE, A = g.vector, g.tensor, g.scalar

    def done(key, ins):
        ins.then_inc(sem[key], 1)
        cnt[key] += 1
        return cnt[key]

    def ts(out, in0, s1, s2, *ops):
        return done("v", V.tensor_scalar(out, in0, s1, s2, *ops))

    def copy(out, in_):
        return done("v", V.tensor_copy(out, in_))

    def vw(n):
        V.wait_ge(sem.v, n)

    def mm(n_v, out, lhsT, rhs, start=True, stop=True):
        if n_v:
            PE.wait_ge(sem.v, n_v)
        return done("pe", PE.matmul(out, lhsT, rhs, start, stop))

    maps = chain(f) if is_rank else list(TEAMS[team][0][1:])
    comps = [m for m in maps if m >= N]
    late = comps[:1] + [m for m in comps[1:] if len(COMPS[m - N][1]) > 2]
    nc = 2 if is_rank else 32 // TEAMS[team][2]
    w = 16 * nc

    def straight_from(m):
        return m < N and topo.may_write(cores[m], core)

    if is_rank:
        if f > 0:
            g.sync.dma_start(T.raw[:, :], T.bp[:, :]).then_inc(sem.dbp, 16)
        if f == TOP:
            g.sync.dma_start(T.wr[0:16, :], T.st[:, :]).then_inc(sem.dst, 16)
        else:
            for k in range(8):
                q = A if k % 2 else g.sync
                q.dma_start(T.wr[16 * k:16 * k + 16, 0:2], T.st[:, 2 * k:2 * k + 2]).then_inc(sem.dst, 16)
        g.sync.dma_start(T.tb[:, :], T.tab[:, :]).then_inc(sem.dtab, 16)

    done("gi", g.iota(T.pidx[:, :], [[0, 1]], 0, 1))
    if not is_rank:
        done("gi", g.iota(T.coi[:, 0:nc], [[2, nc]], 1, 0))
    for t, pattern, mul in ((T.i_r, [[0, 8], [1, 16]], 0), (T.i_g, [[1, 8], [0, 16]], 0)) + (
            () if is_rank else ((T.df, [[0, 8], [8, 16]], -1), (T.i_q, [[1, 8], [8, 16]], -1))):
        done("gi", g.iota(t[:, :], pattern, 0, mul, allow_small_or_imprecise_dtypes=True))

    n_sent = 0 if is_rank else run_relay(g, core, cores, teams, T, topo, off_mask)
    if is_rank and f > 0:
        straight, relay, groups = receivers(f, cores, topo, teams)
        V.wait_ge(sem.dbp, 16)
        ts(T.sp[:, 0:64:2], T.raw[:, :], 3, 510, Op.arith_shift_right, Op.bitwise_and)
        n = ts(T.sp[:, 1:64:2], T.raw[:, :], 15, None, Op.bitwise_and)
        vw(n)
        g.wait_ge(sem.v, copy(land(T, f), T.sp[:, :]))
        calls = [[relay]] if groups and all(relay not in grp for grp in straight) else []
        if groups and straight and straight[0][0] not in cores and all(d in cores for grp in groups for d in grp):
            calls = [straight.pop(0)] + calls
        for grp in calls + straight:
            n_sent += send(g, core, grp, f, T, topo, off_mask)

    V.wait_ge(sem.gi, 3 if is_rank else 2)
    ts(T.pgr[:, 0:1], T.pidx[:, :], 4, None, Op.arith_shift_right)
    ts(T.pgr[:, 1:2], T.pidx[:, :], 15, None, Op.bitwise_and)
    n_rpc = 0
    if is_rank:
        if comps:
            g.wait_ge(sem.v, done("v", V.memset(T.ones[:, :], 1.0)))
            for k in range(0, 8, 2):
                n_rpc = done("gi", g.affine_select(T.rpc[:, 128 * k:128 * k + 256], T.ones[:, :],
                                                   [[-16, 2], [0, 8], [-1, 16]], Op.is_equal, 0.0, -16 * k, 1))
        ts(T.pgr[:, 3:4], T.pidx[:, :], 4, 1, Op.arith_shift_right, Op.bitwise_and)
        n = copy(T.pgr[:, 2:3], T.pidx[:, :])
    else:
        copy(T.cof[:, 0:nc], T.coi[:, 0:nc])
        ts(T.pgr[:, 2:3], T.pidx[:, :], 3, None, Op.arith_shift_right)
        n = ts(T.pgr[:, 3:4], T.pidx[:, :], 7, None, Op.bitwise_and)
    vw(n)
    n_col = copy(T.col[:, :], T.pgr[:, :])
    pg, pr, pp = T.col[:, 0:1], T.col[:, 1:2], T.col[:, 2:3]
    iw = T.i_r[:, 0:w]
    vw(n_col)
    n_df = 0
    if is_rank:
        ts(T.dg[:, 0:w], iw, pr, None, Op.is_equal)
        n_df = ts(T.df[:, :], T.i_r[:, :], 8.0, pp, Op.mult, Op.subtract)
        ts(T.bd[:, :], T.i_g[:, :], pg, None, Op.is_equal)

    def spread_consts():
        if n_df:
            vw(n_df)
        for k in range(8):
            n = ts(T.rp[:, 128 * k:128 * k + 128], T.df[:, :], -float(k), None, Op.is_equal)
        return n

    def scan_consts():
        n = ts(T.r1[:, :], pr, 1.0, None, Op.add)
        ts(T.prl[:, :], pr, LIFT, None, Op.add)
        ts(T.ct1[:, 0:w], iw, pr, None, Op.not_equal)
        vw(n)
        ts(T.sc1[:, :], pr, 15.0, 1.0 - 1.0 / FAR, Op.is_equal, Op.mult)
        n = ts(T.ct2[:, 0:w], iw, T.r1[:, :], FAR, Op.is_equal, Op.mult)
        vw(n)
        done("v", V.tensor_tensor(T.ct[:, 0:w], T.ct1[:, 0:w], T.ct2[:, 0:w], Op.add))
        return ts(T.scl[:, :], T.sc1[:, :], 1.0 / FAR, None, Op.add)

    def end_consts():
        if f == TOP:
            ts(T.ex[0:16, :], T.i_r[0:16, :], T.col[0:16, 1:2], None, Op.is_equal)
            return ts(T.ex8[0:16, :], T.i_r[0:16, :], T.col[0:16, 1:2], 8.0, Op.is_equal, Op.mult)
        ts(T.sel[:, :], T.i_r[:, 0:128:8], 0.125, T.col[:, 3:4], Op.mult, Op.is_equal)
        ts(T.ex[0:w, :], T.i_r[0:w, :], T.col[0:w, 1:2], 8.0, Op.is_equal, Op.mult)
        return ts(T.ex[w:2 * w, :], T.i_r[w:2 * w, :], T.col[w:2 * w, 1:2], None, Op.is_equal)

    n_rp = n_reord = n_state = n_fl = 0
    if not is_rank:
        V.wait_ge(sem.gi, 4)
        ts(T.dgx[:, 0:w], iw, T.col[:, 2:3], None, Op.is_equal)
        ts(T.bdx[:, :], T.i_g[:, :], T.col[:, 3:4], None, Op.is_equal)
        ts(T.bd[:, :], T.i_g[:, :], pg, None, Op.is_equal)
        n_state = scan_consts()
        V.wait_ge(sem.gi, 6)
        n_reord = ts(T.reord[:, :], T.i_q[:, :], 0.0, None, Op.is_equal)
        n_rp = spread_consts()
    elif f == TOP:
        V.wait_ge(sem.dst, 16)
        ts(T.wsp[0:16, 0:16], T.wr[0:16, :], 3, 510, Op.arith_shift_right, Op.bitwise_and)
        n = ts(T.wsp[0:16, 16:32], T.wr[0:16, :], 15, None, Op.bitwise_and)
        vw(n)
        copy(T.fl[0:16, :], T.wsp[0:16, :])
    else:
        V.wait_ge(sem.dst, 128)
        ts(T.wsp[:, 0:2], T.wr[:, 0:2], 3, 510, Op.arith_shift_right, Op.bitwise_and)
        n = ts(T.wsp[:, 2:4], T.wr[:, 0:2], 15, None, Op.bitwise_and)
        vw(n)
        copy(T.offs[:, 0:2], T.wsp[:, 0:2])
        n = copy(T.lof[:, :], T.wsp[:, 2:4])
        vw(n)
        ts(T.rl[:, 0:16], T.dg[:, 0:16], T.lof[:, 0:1], None, Op.mult)
        n = ts(T.rl[:, 16:32], T.dg[:, 16:32], T.lof[:, 1:2], None, Op.mult)
        n_rl = mm(n, T.p_l[:, 0:32], T.bd[:, :], T.rl[:, 0:32])
        n_rp = spread_consts()
        V.wait_ge(sem.pe, n_rl)
        ts(T.mk[:, 0:32], T.p_l[:, 0:32], pr, None, Op.is_equal)
        scan_consts()
        n_state = ts(T.gs[:, :], T.i_g[:, 0:128:8], pg, None, Op.is_equal)
    soon = bool(maps) and straight_from(maps[0])
    if is_rank and not soon:
        n_fl = end_consts()

    if maps:
        banks = {"next": 0}
        bank_free = [("a", 0)] * 4
        wready = {}

        def spread(m, parts, both):
            if m >= N:
                PE.wait_ge(sem.gi, n_rpc)
            PE.wait_ge(sem["m%d" % m], arrived if m < N else arrived * TEAMS[COMPS[m - N][0]][2])
            ready = {}
            per = 8 // parts
            ww = 64 * per
            mat = T.rp if m < N else T.rpc
            for h in range(parts):
                b = banks["next"]
                banks["next"] = (b + 1) % 4
                key, val = bank_free[b]
                if val:
                    PE.wait_ge(sem[key], val)
                ps = T["p_r%d" % b]
                n_pe = 0
                for k in range(per):
                    kk = per * h + k
                    n_pe = mm(0, ps[:, 64 * k:64 * k + 64], mat[:, 128 * kk:128 * kk + 128], land(T, m))
                dst = win(T, m, ww * h, ww * h + ww)
                if both and h % 2:
                    V.wait_ge(sem.pe, n_pe)
                    bank_free[b] = ("v", copy(dst, ps[:, 0:ww]))
                else:
                    A.wait_ge(sem.pe, n_pe)
                    bank_free[b] = ("a", done("a", A.activation(dst, ps[:, 0:ww], Act.Copy)))
                ready[bank_free[b][0]] = bank_free[b][1]
            wready[m] = ready

        n_rl = n_o = 0
        if not is_rank:
            m0 = TEAMS[team][0][0]
            base = 64 * m0 + 2 * nc * part
            mine = T.land[:, base:base + 2 * nc]
            PE.wait_ge(sem.v, n_reord)
            PE.wait_ge(sem["m%d" % m0], arrived)
            n_o = mm(0, T.p_h[:, 0:2 * nc], T.reord[:, :], mine)
            V.wait_ge(sem["m%d" % m0], arrived)
            vw(n_state)
            n_rl = done("v", V.tensor_tensor(T.rl[:, 0:w], mine.indirect(T.cof[:, 0:nc]), T.dgx[:, 0:w], Op.mult))
            V.wait_ge(sem.pe, n_o)
            copy(T.offs[:, 0:nc], T.p_h[:, 0:2 * nc:2])
        PE.wait_ge(sem.v, n_rp)
        todo = list(maps)
        for m in [x for x in todo[:EARLY] if straight_from(x)]:
            todo.remove(m)
            first = m == maps[0]
            spread(m, 4 if first else 2, first)
            if not is_rank and first:
                n_pl = mm(n_rl, T.p_l[:, 0:w], T.bdx[:, :], T.rl[:, 0:w])
                V.wait_ge(sem.pe, n_pl)
                n_state = ts(T.mk[:, 0:w], T.p_l[:, 0:w], pr, None, Op.is_equal)
        fast = {"next": True}

        def spread_next(idle):
            x = todo.pop(0)
            quick = fast["next"] or idle
            fast["next"] = False
            spread(x, 4 if quick else 2, quick)

        nh = nl = 0
        for i in range(len(maps)):
            m = maps[i]
            while m not in wready:
                spread_next(True)
            if i > 0 and todo and todo[0] == maps[min(i + 1, len(maps) - 1)] and todo[0] not in late:
                spread_next(False)
            for key in wready[m]:
                V.wait_ge(sem[key], wready[m][key])
            vw(n_state)
            o = T.offs[:, 0:nc]
            nh = done("v", V.tensor_tensor(T.xx[:, 0:w], win(T, m, 0, 511).indirect(o), T.mk[:, 0:w], Op.mult))
            nl = done("v", V.tensor_tensor(T.xx[:, w:2 * w], win(T, m, 1, 512).indirect(o), T.mk[:, 0:w], Op.mult))
            out = [x for x in range(len(COMPS)) if not is_rank and COMPS[x][0] == team and len(COMPS[x][1]) == i + 2]
            if i + 1 < len(maps) or out:
                h = mm(nh, T.p_h[:, 0:w], T.bd[:, :], T.xx[:, 0:w])
                l = mm(nl, T.p_l[:, 0:w], T.bd[:, :], T.xx[:, w:2 * w])
                V.wait_ge(sem.pe, h)
                n = done("v", V.tensor_tensor_scan(T.scn[:, 0:w], T.ct[:, 0:w], T.p_h[:, 0:w], 0.0, Op.mult, Op.add))
                V.wait_ge(sem.pe, l)
            if i + 1 < len(maps):
                ts(T.mk[:, 0:w], T.p_l[:, 0:w], T.prl[:, :] if m >= N else pr, None, Op.is_equal)
                vw(n)
                n_state = ts(T.offs[:, 0:nc], T.scn[:, 15:w:16], T.scl[:, :], None, Op.mult)
            if i == 0 and is_rank and soon:
                end_consts()
            for x in out:
                e = 16 * x
                A.wait_ge(sem.v, n)
                n_eh = done("a", A.activation(T.em[:, e:e + 2 * nc:2], T.scn[:, 15:w:16], Act.Copy,
                                              scale=T.scl[:, :]))
                n2 = done("v", V.tensor_tensor_scan(T.scn[:, w:2 * w], T.ct[:, 0:w], T.p_l[:, 0:w], 0.0,
                                                    Op.mult, Op.add))
                vw(n2)
                n = ts(T.em[:, e + 1:e + 2 * nc:2], T.scn[:, w + 15:2 * w:16], T.scl[:, :], LIFT, Op.mult, Op.add)
                g.wait_ge(sem.a, n_eh)
                g.wait_ge(sem.v, n)
                a = 64 * (N + x) + 2 * nc * part
                ranks = [cores[r] for r in COMPS[x][2]]
                for k in range(0, len(ranks), 2):
                    n_sent += send(g, core, ranks[k:k + 2], N + x, T, topo, off_mask,
                                   T.em[:, e:e + 2 * nc], T.land[:, a:a + 2 * nc])
        if not is_rank:
            for key in ("v", "pe", "a", "gi"):
                g.wait_ge(sem[key], cnt[key])
            g.wait_ge(sem.sa, n_sent)
            return
        n = mm(nl, T.p_f[0:2 * w, 0:16], T.xx[:, 0:2 * w], T.gs[:, :])
        V.wait_ge(sem.pe, n)
        n_fl = done("v", V.tensor_tensor(T.fl[0:2 * w, 0:16], T.p_f[0:2 * w, 0:16], T.sel[0:2 * w, :], Op.mult))

    if maps:
        n = mm(n_fl, T.p_g[:, 0:16], T.ex[0:2 * w, :], T.fl[0:2 * w, 0:16])
    else:
        mm(n_fl, T.p_g[:, 0:16], T.ex8[0:16, :], T.fl[0:16, 0:16], True, False)
        n = mm(0, T.p_g[:, 0:16], T.ex[0:16, :], T.fl[0:16, 16:32], False, True)
    V.wait_ge(sem.pe, n)
    n_fo = ts(T.fo[:, :], T.p_g[:, 0:16], -LIFT if maps and maps[-1] >= N else 0.0, None, Op.add)

    V.wait_ge(sem.dtab, 16)
    vw(n_fo)
    n_ya = copy(T.ya[:, :], T.tb[:, :].indirect(T.fo[:, 0:8]))
    A.wait_ge(sem.dtab, 16)
    A.wait_ge(sem.v, n_fo)
    n_yb = done("a", A.activation(T.yb[:, :], T.tb[:, :].indirect(T.fo[:, 8:16]), Act.Copy))
    g.sync.wait_ge(sem.v, n_ya)
    g.sync.dma_start(T.y[:, 0:128], T.ya[:, :]).then_inc(sem.dya, 16)
    A.wait_ge(sem.a, n_yb)
    A.dma_start(T.y[:, 128:256], T.yb[:, :]).then_inc(sem.dyb, 16)

    for key in ("v", "pe", "a", "gi"):
        g.wait_ge(sem[key], cnt[key])
    if n_sent:
        g.wait_ge(sem.sa, n_sent)
    g.wait_ge(sem.dya, 16)
    g.wait_ge(sem.dyb, 16)
